import numpy as np, ml_dtypes
CORES = [6,15,38,47]
N = 4
BF = ml_dtypes.bfloat16
L, S, Q = 512, 3, 1536
def packed(rng, st):
    fr = np.diff(np.append(st, 2048)); sy = rng.permutation(256)[:len(st)]
    return np.stack([np.repeat(2048 * (fr - 1) + st, fr), np.repeat(sy, fr)])
def model(rng, n):
    return packed(rng, np.concatenate([[0], np.sort(rng.integers(0, 2048 - 8 * n + 1, n - 1)) + 8 * np.arange(1, n)]).astype(np.int64))
def both(m):
    return {"models": np.ascontiguousarray(m[:, :, 0]).astype(np.int32), "letters": np.ascontiguousarray(m[:, :, 1]).astype(np.int32)}
def models_of(rng, n):
    return both(np.stack([np.stack([model(rng, int(n[r, g])) for g in range(8)]) for r in range(N)]))
def some_states(rng):
    return np.clip(np.exp2(12 + 8 * rng.random((N, 8, L))), 4096, 1048575).astype(np.int32)
def some_bytes(rng):
    return rng.integers(0, 256, (N, 8, Q)).astype(np.int32)
def same(p):
    return np.repeat(p[None], N, axis=0).astype(np.int32)
def some_places(rng):
    return same(np.stack([rng.permutation(N * Q) for g in range(8)]))
def setup_inputs(rng):
    n = np.exp2(1 + 6.5 * rng.random((N, 8))).astype(np.int64); n[:, rng.integers(0, 8)] = 256
    m = models_of(rng, n)
    return {"states": some_states(rng), "models": m["models"], "letters": m["letters"], "stock": some_bytes(rng), "places": some_places(rng)}
def setup_inputs_every(rng):
    x = some_states(rng); x[:, :, 0] = 4096; x[:, :, L - 1] = 1048575
    m = models_of(rng, np.full((N, 8), 256)); p = some_places(rng); g = rng.permutation(8)
    p[:, g[0]] = np.arange(N * Q); p[:, g[1]] = np.arange(N * Q)[::-1]
    return {"states": x, "models": m["models"], "letters": m["letters"], "stock": some_bytes(rng), "places": p}
def setup_inputs_dry(rng):
    d = setup_inputs(rng); n = np.exp2(1 + 6.5 * rng.random((N, 8))).astype(np.int64); g = rng.permutation(8); p = rng.permutation(N)
    n[:, g[:3]] = 1
    for i in range(5):
        n[p[i % N], g[3 + i]] = 1
    d.update(models_of(rng, n)); return d
def setup_inputs_edge(rng):
    k = 2 ** rng.integers(4, 11, (N, 8, 1)); up = 4096 // k; a = rng.integers(0, 2048, (N, 8, L)) // k * k
    kind = rng.integers(0, 4, (N, 8, L)); kind[:, :, :4] = np.arange(4)
    x = np.where(kind == 0, 2048 * up + a, np.where(kind == 1, 2048 * (up - 1) + a + k - 1, np.where(kind == 2, 4096, 1048575)))
    m = both(np.stack([np.stack([packed(rng, np.arange(0, 2048, int(k[r, g, 0]))) for g in range(8)]) for r in range(N)]))
    return {"states": x.astype(np.int32), "models": m["models"], "letters": m["letters"], "stock": (255 * rng.integers(0, 2, (N, 8, Q))).astype(np.int32), "places": some_places(rng)}
def setup_inputs_few(rng):
    x = rng.integers(2 ** 19, 2 ** 20, (N, 8, L)); x[:, :, 0] = rng.integers(4096, 8192, (N, 8)); x[:, :, L - 1] = rng.integers(4096, 8192, (N, 8)); x[:, :, 1] = rng.integers(8192, 16384, (N, 8))
    p = rng.permutation(N); m = both(np.stack([np.stack([packed(rng, np.arange(0, 2048, 8 if p[g % N] == r else 1024)) for g in range(8)]) for r in range(N)]))
    return {"states": x.astype(np.int32), "models": m["models"], "letters": m["letters"], "stock": some_bytes(rng), "places": some_places(rng)}
def setup_inputs_spread(rng):
    slot = np.arange(2048); e = np.floor((slot + 1) * rng.random((N, 8, 2048)) ** 3).astype(np.int64); e = np.minimum(e, slot)
    lo = np.maximum(e, 7); w = np.minimum(lo + np.floor((2048 - lo) * rng.random((N, 8, 2048)) ** 4).astype(np.int64), 2047)
    m = 2048 * w + slot - e
    b = np.minimum(np.floor(256 * rng.random((N, 8, Q)) ** 6), 255)
    return {"states": some_states(rng), "models": m.astype(np.int32), "letters": rng.integers(0, 256, (N, 8, 2048)).astype(np.int32), "stock": b.astype(np.int32), "places": some_places(rng)}
def check_inputs(d):
    x, t, a, b, p = d["states"], d["models"].astype(np.int64), d["letters"], d["stock"], d["places"]; bad = []; slot = np.arange(2048)
    if not ((x >= 4096) & (x < 1048576)).all(): bad.append("states")
    if not ((t >= 14336) & (t < 4194304) & ((t & 2047) <= slot) & (slot <= (t & 2047) + (t >> 11))).all(): bad.append("models")
    if not ((a >= 0) & (a < 256)).all(): bad.append("letters")
    if not ((b >= 0) & (b < 256)).all(): bad.append("stock")
    if not ((np.sort(p, axis=2) == np.arange(N * Q)).all() and (p == p[:1]).all()): bad.append("places")
    return bad
def whole(b):
    return np.ascontiguousarray(b.transpose(1, 0, 2)).reshape(8, -1)
def line(v, s):
    return np.ascontiguousarray(v.transpose(1, 2, 0)).reshape(8, -1)
def unline(u, s):
    return u.reshape(8, L, N).transpose(2, 0, 1)
def reference(states, models, letters, stock, places):
    x = states.astype(np.int64); t = models.astype(np.int64); pool = whole(stock.astype(np.int64)); seq = places[0].astype(np.int64)
    syms = np.zeros((N, 8, S * L), np.int32); used = np.zeros(8, np.int64)
    for s in range(S):
        slot = x & 2047; e = np.take_along_axis(t, slot, 2)
        syms[:, :, s * L:(s + 1) * L] = np.take_along_axis(letters, slot, 2)
        x = ((e >> 11) + 1) * (x >> 11) + slot - (e & 2047)
        reads = x < 4096; w = line(reads, s).astype(np.int64)
        at = used[:, None] + np.add.accumulate(w, axis=1) - w
        x = np.where(reads, 256 * x + unline(np.take_along_axis(pool, np.take_along_axis(seq, at, 1), 1), s), x)
        used = used + np.add.reduce(w, axis=1)
    return {"syms": np.asarray(syms, np.float32), "last": np.asarray(x, np.float32)}

@@ -1,0 +1,356 @@
+from concourse.bass import DstId, RemoteDMATransfer
+from concourse.mybir import dt, AluOpType, AxisListType, ActivationFunctionType
+
+N, L, S, Q = 4, 512, 3, 1536
+SCRATCH = {
+    "stin": ("sbuf", [128, 96], "int32"),
+    "stb": ("sbuf", [128, 96], "bfloat16"),
+    "stk": ("dram", [4, 128, 96], "bfloat16"),
+    "stw": ("sbuf", [128, 6144], "bfloat16"),
+    "mi": ("sbuf", [128, 2, 64], "int32"),
+    "le": ("sbuf", [128, 2, 64], "int32"),
+    "mc": ("sbuf", [128, 2, 64], "int32"),
+    "mf": ("sbuf", [128, 2, 64], "int32"),
+    "qf": ("sbuf", [128, 64, 2], "float32"),
+    "qd": ("sbuf", [128, 64, 2], "float32"),
+    "ql": ("sbuf", [128, 64, 2], "float32"),
+    "win": ("sbuf", [128, 4096], "float32"),
+    "sl": ("sbuf", [128, 64], "int32"),
+    "slm": ("sbuf", [128, 64], "int32"),
+    "hi": ("sbuf", [128, 8], "int32"),
+    "hf": ("sbuf", [128, 8], "float32"),
+    "si": ("sbuf", [128, 32], "int32"),
+    "sf": ("sbuf", [128, 32], "float32"),
+    "sx": ("sbuf", [128, 32], "float32"),
+    "x": ("sbuf", [128, 32], "int32"),
+    "offi": ("sbuf", [128, 32], "int32"),
+    "offu": ("sbuf", [128, 32], "uint16"),
+    "xs": ("sbuf", [128, 32], "float32"),
+    "G": ("sbuf", [128, 512], "float32"),
+    "TT": ("sbuf", [128, 512], "float32"),
+    "m": ("sbuf", [128, 32], "float32"),
+    "x1": ("sbuf", [128, 32], "float32"),
+    "F": ("sbuf", [128, 32], "bfloat16"),
+    "ir": ("sbuf", [128, 4, 104], "bfloat16"),
+    "tm": ("sbuf", [128, 32], "float32"),
+    "pa": ("sbuf", [128, 32], "float32"),
+    "pb": ("sbuf", [128, 32], "float32"),
+    "posu": ("sbuf", [128, 32], "uint16"),
+    "G2": ("sbuf", [128, 512], "bfloat16"),
+    "T2": ("sbuf", [128, 512], "bfloat16"),
+    "pl": ("sbuf", [128, 3, 2, 4, 16], "int32"),
+    "Z": ("sbuf", [128, 4, 32], "float32"),
+    "ZT": ("sbuf", [128, 128], "float32"),
+    "lu": ("sbuf", [128, 384], "uint16"),
+    "W": ("sbuf", [128, 6160], "bfloat16"),
+    "syt": ("sbuf", [128, 96], "float32"),
+    "xl": ("sbuf", [128, 32], "float32"),
+    "xlt": ("sbuf", [128, 32], "float32"),
+    "onesf": ("sbuf", [128, 128], "float32"),
+    "onesb": ("sbuf", [128, 128], "bfloat16"),
+    "e8": ("sbuf", [128, 128], "bfloat16"),
+    "zb": ("sbuf", [128, 512], "bfloat16"),
+    "P0": ("sbuf", [128, 128], "float32"),
+    "P1": ("sbuf", [128, 128], "float32"),
+    "P2": ("sbuf", [128, 128], "float32"),
+    "P3": ("sbuf", [128, 128], "float32"),
+    "blk": ("sbuf", [128, 128], "bfloat16"),
+    "blk2": ("sbuf", [128, 128], "bfloat16"),
+    "A1": ("sbuf", [128, 128], "bfloat16"),
+    "A2": ("sbuf", [128, 128], "bfloat16"),
+    "A3": ("sbuf", [128, 128], "bfloat16"),
+    "A4": ("sbuf", [128, 128], "bfloat16"),
+    "E8": ("sbuf", [128, 128], "bfloat16"),
+    "pxs": ("psum", [128, 512], "float32"),
+    "pp": ("psum", [128, 512], "float32"),
+    "ppos": ("psum", [128, 512], "float32"),
+}
+NDMA = 48
+SEMAPHORES = (["sv", "ss", "sp", "sg", "loc"] + ["d%d" % i for i in range(NDMA)] + ["ak%d" % r for r in range(N)]
+              + ["ai%d_%d" % (r, s) for r in range(N) for s in range(S)])
+
+VM = 14
+VB = 16
+VO = 48
+
+
+def rank_program(g, core, T, topo):
+    me = T.rank_of(core)
+    if me is None:
+        return
+    A = AluOpType
+    COPY = ActivationFunctionType.Copy
+    queues = {"v": g.vector, "s": g.scalar, "p": g.tensor, "g": g, "y": g.sync}
+    own = {"v": "sv", "s": "ss", "p": "sp", "g": "sg"}
+    count, known, wrote, read = {}, {}, {}, {}
+    ndma = [0]
+
+    def need(q, ev):
+        sem, n = ev[0], ev[1]
+        if known.get((q, sem), 0) < n:
+            queues[q].wait_ge(T.sem[sem], n)
+            known[(q, sem)] = n
+
+    def E(q, call, reads=(), writes=(), deps=(), dma=False):
+        evs = list(deps)
+        for r in reads:
+            evs += wrote.get(r, [])
+        for w in writes:
+            evs += [e for e in wrote.get(w, [])]
+            evs += [e for e in read.get(w, []) if e[2] != q or e[0] != own.get(q)]
+        for e in evs:
+            if q == "p" and e[0] == "sp":
+                continue
+            need(q, e)
+        ins = call()
+        if dma:
+            sem = "d%d" % ndma[0]
+            ndma[0] += 1
+            ins.then_inc(T.sem[sem], 16)
+            ev = (sem, 16, q)
+            count[sem] = 16
+        else:
+            sem = own[q]
+            count[sem] = count.get(sem, 0) + 1
+            ins.then_inc(T.sem[sem], 1)
+            ev = (sem, count[sem], q)
+        for r in reads:
+            read.setdefault(r, []).append(ev)
+        for w in writes:
+            wrote[w] = [ev]
+            read[w] = []
+        return ev
+
+    def D(q, out, in_, reads=(), writes=(), deps=()):
+        return E(q, lambda: queues[q].dma_start(out, in_), reads, writes, deps, True)
+
+    V = g.vector
+
+    def vcopy(out, in_, reads, writes, deps=()):
+        return E("v", lambda: V.tensor_copy(out, in_), reads, writes, deps)
+
+    def vfill(ap, c, w):
+        return E("v", lambda: V.memset(ap, c), (), [w])
+
+    def vts(out, in0, s1, op0, reads, writes, deps=(), s2=None, op1=None):
+        if op1 is None:
+            return E("v", lambda: V.tensor_scalar(out, in0, s1, None, op0), reads, writes, deps)
+        return E("v", lambda: V.tensor_scalar(out, in0, s1, s2, op0, op1), reads, writes, deps)
+
+    def vtt(out, a, b, op, reads, writes, deps=()):
+        return E("v", lambda: V.tensor_tensor(out, a, b, op), reads, writes, deps)
+
+    def vtr(out, in_, reads, writes):
+        return E("v", lambda: V.transpose(out, in_), reads, writes)
+
+    def scopy(out, in_, reads, writes, deps=(), scale=1.0):
+        return E("s", lambda: g.scalar.activation(out, in_, COPY, scale=scale), reads, writes, deps)
+
+    cores = list(T.cores)
+
+    def hops(r):
+        a, b = topo.chip(core), topo.chip(cores[r])
+        return 0 if a == b else (1 if topo.mates(a, b) or topo.same_plane(a, b) else 2)
+
+    near = sorted([r for r in range(N) if r != me], key=hops)
+    far = near[::-1]
+    engs = [e for e in topo.engines(core, cores[far[0]]) if all(e in topo.engines(core, cores[r]) for r in far)]
+    emask = 0
+    for e in engs:
+        emask |= 1 << e
+    ne = len(engs)
+    sent = [0]
+
+    def send(src, dst, sem):
+        ids = []
+        for r in far:
+            ad = topo.addr(cores[r])
+            ids.append(DstId(rid=ad[0], pnc=ad[1]))
+        g.remote_dma_fused([RemoteDMATransfer(dst_ids=ids, dma_engine_mask=emask, remote_sem=T.sem[sem],
+                                              srcs=[src], dsts=[dst for r in far])], local_sem=T.sem.loc)
+        sent[0] += ne
+
+    D("y", T.stin[:], T.stock[:], (), ["stin"])
+    for h in range(2):
+        D("s", T.mi[:, h, :], T.models[h::2, :], (), ["mi%d" % h])
+    for h in range(2):
+        D("y", T.si[h::2, :], T.states[h::2, :], (), ["si%d" % h])
+    for h in range(2):
+        D("y", T.le[:, h, :], T.letters[h::2, :], (), ["le%d" % h])
+
+    def load_places(B):
+        for w in range(2):
+            D("y", T.pl[:, B, w], T.places[w::2, 2048 * B:2048 * B + 2048], (), ["pl%d_%d" % (B, w)])
+
+    load_places(0)
+
+    vfill(T.onesf[:], 1.0, "onesf")
+    f0 = vfill(T.win[:, 0:512], 0.0, "wa")
+    vfill(T.onesb[:], 1.0, "onesb")
+    vfill(T.e8[:], 8192.0, "e8")
+    vfill(T.zb[:], 0.0, "zb")
+    E("g", lambda: g.iota(T.sl[:], [[1, 64]], 0, 64), (), ["sl"])
+    for k, base in enumerate((0, -1000, -16, -1016)):
+        out = T["P%d" % k]
+        E("g", lambda: g.affine_select(out[:], T.onesf[:], [[-32, 4], [1000, 2], [-1, 16]], A.is_equal, 0.0, base, 1),
+          ["onesf"], ["P%d" % k])
+    fw = [f0]
+    for k in range(3):
+        fw.append(scopy(T.win[:, 2560 + 512 * k:3072 + 512 * k], T.win[:, 0:512], ["wa"], ["wc%d" % k]))
+    fw.append(vfill(T.win[:, 512:2560], 0.0, "wb"))
+    vfill(T.ir[:, :, 0:8], 0.0, "irz")
+    vfill(T.W[:, 0:16], 0.0, "wz")
+
+    vts(T.stb[:], T.stin[:], 2.0, A.mult, ["stin"], ["stb"])
+    need("g", wrote["stb"][0])
+    send(T.stb[:], T.stk[me], "ak%d" % me)
+
+    E("g", lambda: g.affine_select(T.blk[:], T.onesb[:], [[-16, 8], [0, 16]], A.is_ge, 0.0, 0, 1), ["onesb"], ["blk"])
+    E("g", lambda: g.affine_select(T.blk2[:], T.blk[:], [[16, 8], [0, 16]], A.is_ge, 0.0, 15, -1), ["blk"], ["blk2"])
+    E("g", lambda: g.affine_select(T.A3[:], T.blk2[:], [[1, 128]], A.is_gt, 0.0, 0, -1), ["blk2"], ["A3"])
+    E("g", lambda: g.affine_select(T.A4[:], T.blk2[:], [[-1, 128]], A.is_ge, 0.0, 0, 1), ["blk2"], ["A4"])
+    E("g", lambda: g.affine_select(T.E8[:], T.e8[:], [[-1, 128]], A.is_equal, 0.0, 0, 1), ["e8"], ["E8"])
+    if me > 0:
+        E("g", lambda: g.affine_select(T.A1[:], T.blk2[:], [[1, 128]], A.is_ge, 0.0, 0, -1), ["blk2"], ["A1"])
+        E("g", lambda: g.affine_select(T.A2[:], T.blk2[:], [[-1, 128]], A.is_gt, 0.0, 0, 1), ["blk2"], ["A2"])
+
+    vts(T.slm[:], T.sl[:], 2047, A.bitwise_and, ["sl"], ["slm"])
+    vts(T.mc[:], T.mi[:], 2047, A.bitwise_and, ["mi0", "mi1"], ["mc"])
+    vts(T.mf[:], T.mi[:], 11, A.logical_shift_right, ["mi0", "mi1"], ["mf"])
+    for h in range(2):
+        vtt(T.qd[:, :, h], T.slm[:], T.mc[:, h, :], A.subtract, ["slm", "mc"], ["qd%d" % h])
+    for h in range(2):
+        vts(T.qf[:, :, h], T.mf[:, h, :], 1.0, A.add, ["mf"], ["qf%d" % h], (), 1.0 / 4096, A.mult)
+    wd = []
+    for k, nm in ((1, "qd"), (0, "qf")):
+        for w in range(2):
+            wd.append(D("y", T.win[16 * w + k::32, :], T[nm][:], [nm + "0", nm + "1"], (), fw))
+    for h in range(2):
+        vcopy(T.ql[:, :, h], T.le[:, h, :], ["le%d" % h], ["ql%d" % h])
+    for w in range(2):
+        wd.append(D("y", T.win[16 * w + 2::32, :], T.ql[:], ["ql0", "ql1"], (), fw))
+
+    vcopy(T.sf[:], T.si[:], ["si0", "si1"], ["sf"])
+    vtr(T.sx[:], T.sf[:], ["sf"], ["sx"])
+    for h in range(2):
+        vts(T.x[:, h::2], T.sx[:, h::2], 2.0, A.mult, ["sx"], ["x%d" % h], (), float(h), A.add)
+    vts(T.hi[:, 0:1], T.sl[:, 0:1], 10, A.logical_shift_right, ["sl"], ["hi"], (), 1, A.bitwise_and)
+    vcopy(T.hf[:, 0:1], T.hi[:, 0:1], ["hi"], ["hf"])
+
+    def swap(out, w, src, r):
+        for c in range(2):
+            for i in range(2):
+                E("p", lambda: g.tensor.matmul(out[:, c:32:2], T["P%d" % (2 * c + i)][:] if False else T["P%d" % (2 * c if False else (c * 2 + i))][:],
+                                               src[:, i:32:2], i == 0, i == 1),
+                  [r] + ["P%d" % (c * 2 + i)], [w])
+
+    def start_lookup():
+        vts(T.offi[:], T.x[:], 4095, A.bitwise_and, ["x0", "x1"], ["offi"])
+        vcopy(T.offu[:], T.offi[:], ["offi"], ["offu"])
+
+    def keep_high():
+        vtt(T.xs[:], T.x[:], T.offi[:], A.subtract, ["x0", "x1", "offi"], ["xs"])
+        swap(T.pxs, "pxs", T.xs, "xs")
+
+    start_lookup()
+    keep_high()
+
+    fs = [vfill(T.stw[:, 0:4096], 0.0, "stA")]
+    for k in range(4):
+        fs.append(scopy(T.stw[:, 4096 + 512 * k:4608 + 512 * k], T.zb[:], ["zb"], ["stB%d" % k]))
+    sd = [D("y", T.stw[0::16, Q * me:Q * me + Q], T.stb[:], ["stb"], (), fs)]
+    load_places(1)
+    load_places(2)
+    for r in near:
+        count["ak%d" % r] = ne
+        sd.append(D("y", T.stw[0::16, Q * r:Q * r + Q], T.stk[r], (), (), fs + [("ak%d" % r, ne, "r")]))
+
+    def list_of(B):
+        for w in range(2):
+            vcopy(T.Z[:, :, 16 * w:16 * w + 16], T.pl[:, B, w], ["pl%d_%d" % (B, w)], ["Z%d" % w])
+        for u in range(4):
+            vtr(T.ZT[:, u::4], T.Z[:, u, :], ["Z0", "Z1"], ["ZT%d" % u])
+        vcopy(T.lu[:, 128 * B:128 * B + 128], T.ZT[:], ["ZT%d" % u for u in range(4)], ["lu%d" % B])
+
+    def order(B):
+        w0, c0 = 16 + 2048 * B, 128 * B
+        scopy(T.W[:, w0 + 16 * VO:w0 + 2048], T.stw[:, 0:6144].indirect(T.lu[:, c0 + VO:c0 + 128]),
+              ["lu%d" % B], ["WS%d" % B], sd)
+        vcopy(T.W[:, w0:w0 + 16 * VO], T.stw[:, 0:6144].indirect(T.lu[:, c0:c0 + VO]),
+              ["lu%d" % B], ["WV%d" % B], sd)
+
+    for s in range(S):
+        last = s == S - 1
+        if s > 0:
+            start_lookup()
+        scopy(T.G[:, 16 * VM:512], T.win[:, 0:4096].indirect(T.offu[:, VM:32]), ["offu"], ["GS"], wd)
+        if s > 0:
+            keep_high()
+        vcopy(T.G[:, 0:16 * VM], T.win[:, 0:4096].indirect(T.offu[:, 0:VM]), ["offu"], ["GV"], wd)
+        vtr(T.TT[:, 0:16 * VM], T.G[:, 0:16 * VM], ["GV"], ["TV"])
+        vtr(T.TT[:, 16 * VM:512], T.G[:, 16 * VM:512], ["GS"], ["TS"])
+        vtt(T.m[:], T.TT[:, 0::16], T.pxs[:, 0:32], A.mult, ["TV", "TS", "pxs"], ["m"])
+        vtt(T.x1[:], T.m[:], T.TT[:, 1::16], A.add, ["m", "TV", "TS"], ["xn"])
+        vts(T.F[:], T.x1[:], 4096.0, A.is_lt, ["xn"], ["F"])
+        c0 = 8 + 32 * s
+        prev = "irz" if s == 0 else "ir%d_%d" % (me, s - 1)
+        E("v", lambda: V.tensor_tensor_scan(T.ir[:, me, c0:c0 + 32], T.F[:], T.zb[:, 0:32],
+                                            T.ir[:, me, c0 - 1:c0], A.add, A.add),
+          ["F", "zb", prev], ["ir%d_%d" % (me, s)])
+        need("g", wrote["ir%d_%d" % (me, s)][0])
+        send(T.ir[:, me, c0:c0 + 32], T.ir[:, me, c0:c0 + 32], "ai%d_%d" % (me, s))
+
+        def count_in(r, first, final):
+            hi, lo = ("A1", "A2") if r < me else ("A3", "A4")
+            rd = ["ir%d_%d" % (r, s), "irz"] + ([] if s == 0 else ["ir%d_%d" % (r, s - 1)])
+            E("p", lambda: g.tensor.matmul(T.ppos[:, 0:32], T[hi][:], T.ir[:, r, c0:c0 + 32], first, False),
+              rd + [hi], ["ppos"])
+            E("p", lambda: g.tensor.matmul(T.ppos[:, 0:32], T[lo][:], T.ir[:, r, c0 - 1:c0 + 31], False, final),
+              rd + [lo], ["ppos"])
+
+        count_in(me, True, False)
+        E("p", lambda: g.tensor.matmul(T.ppos[:, 0:32], T.E8[:], T.F[:], False, False), ["F", "E8"], ["ppos"])
+
+        if s == 0:
+            list_of(0)
+        vts(T.tm[:], T.F[:], 255.0 if last else 510.0, A.mult, ["F"], ["tm"], (), 1.0 if last else 2.0, A.add)
+        vtt(T.pa[:], T.x1[:], T.tm[:], A.mult, ["xn", "tm"], ["pa"])
+        if last:
+            swap(T.pp, "pp", T.pa, "pa")
+        else:
+            vts(T.pb[:], T.pa[:], T.hf[:, 0:1], A.add, ["pa", "hf"], ["pb"])
+            swap(T.pp, "pp", T.pb, "pb")
+        vtr(T.syt[:, 32 * s:32 * s + 32], T.TT[:, 2::16], ["TV", "TS"], ["sy%d" % s])
+        order(s)
+        for w in range(2):
+            D("y", T.syms[w::2, 512 * s:512 * s + 512], T.syt[:, 32 * s + 16 * w:32 * s + 16 * w + 16], ["sy%d" % s])
+        if not last:
+            list_of(s + 1)
+
+        for i, r in enumerate(near):
+            nm = "ai%d_%d" % (r, s)
+            count[nm] = ne
+            wrote["ir%d_%d" % (r, s)] = [(nm, ne, "r")]
+            count_in(r, False, i == N - 2)
+        vts(T.posu[:], T.ppos[:, 0:32], -8176.0, A.add, ["ppos"], ["posu"], (), 0.0, A.max)
+        wr = ["posu", "wz"] + ["WS%d" % B for B in range(s + 1)] + ["WV%d" % B for B in range(s + 1)]
+        win2 = T.W[:, 0:16 + 2048 * (s + 1)]
+        scopy(T.G2[:, 16 * VB:512], win2.indirect(T.posu[:, VB:32]), wr, ["HS"], (), 0.5 if last else 1.0)
+        if last:
+            vts(T.G2[:, 0:16 * VB], win2.indirect(T.posu[:, 0:VB]), 0.5, A.mult, wr, ["HV"])
+        else:
+            vcopy(T.G2[:, 0:16 * VB], win2.indirect(T.posu[:, 0:VB]), wr, ["HV"])
+        vtr(T.T2[:, 0:16 * VB], T.G2[:, 0:16 * VB], ["HV"], ["UV"])
+        vtr(T.T2[:, 16 * VB:512], T.G2[:, 16 * VB:512], ["HS"], ["US"])
+        if not last:
+            vtt(T.x[:], T.T2[:, 0::16], T.pp[:, 0:32], A.add, ["UV", "US", "pp"], ["x0", "x1"])
+        else:
+            vtt(T.xl[:], T.T2[:, 0::16], T.pp[:, 0:32], A.add, ["UV", "US", "pp"], ["xl"])
+            vtr(T.xlt[:], T.xl[:], ["xl"], ["xlt"])
+            for h, q in ((0, "y"), (1, "s")):
+                D(q, T.last[h::2, :], T.xlt[h::2, :], ["xlt"])
+
+    for sem in sorted(count):
+        if max([known.get((q, sem), 0) for q in queues]) < count[sem]:
+            need("y", (sem, count[sem], ""))
+    g.wait_ge(T.sem.loc, sent[0])

@@ -3,75 +3,81 @@ from concourse.mybir import dt, AluOpType, AxisListType, ActivationFunctionType
 
 N, L, S, Q = 4, 512, 3, 1536
 SCRATCH = {
+    "tx2": ("dram", [4, 128, 32], "int32"),
+    "rx2": ("dram", [4, 128, 32], "int32"),
+    "tx1": ("dram", [4, 128, 24], "bfloat16"),
+    "rx1": ("dram", [4, 128, 24], "bfloat16"),
+    "tx0": ("dram", [4, 128, 8], "int32"),
+    "rx0": ("dram", [4, 128, 8], "int32"),
     "stin": ("sbuf", [128, 96], "int32"),
     "stb": ("sbuf", [128, 96], "bfloat16"),
-    "stk": ("dram", [4, 128, 96], "bfloat16"),
+    "sx": ("sbuf", [128, 32], "int32"),
     "stw": ("sbuf", [128, 6144], "bfloat16"),
-    "mi": ("sbuf", [128, 2, 64], "int32"),
-    "le": ("sbuf", [128, 2, 64], "int32"),
-    "mc": ("sbuf", [128, 2, 64], "int32"),
-    "mf": ("sbuf", [128, 2, 64], "int32"),
-    "qf": ("sbuf", [128, 64, 2], "float32"),
-    "qd": ("sbuf", [128, 64, 2], "float32"),
-    "ql": ("sbuf", [128, 64, 2], "float32"),
-    "win": ("sbuf", [128, 4096], "float32"),
-    "sl": ("sbuf", [128, 64], "int32"),
-    "slm": ("sbuf", [128, 64], "int32"),
-    "hi": ("sbuf", [128, 8], "int32"),
-    "hf": ("sbuf", [128, 8], "float32"),
-    "si": ("sbuf", [128, 32], "int32"),
-    "sf": ("sbuf", [128, 32], "float32"),
-    "sx": ("sbuf", [128, 32], "float32"),
+    "win": ("sbuf", [128, 2048], "int32"),
+    "mi": ("sbuf", [128, 128], "int32"),
+    "mc": ("sbuf", [128, 128], "int32"),
+    "mf": ("sbuf", [128, 128], "int32"),
+    "sl": ("sbuf", [128, 128], "int32"),
+    "slm": ("sbuf", [128, 128], "int32"),
+    "qf": ("sbuf", [128, 128], "float32"),
+    "qd": ("sbuf", [128, 128], "float32"),
+    "li": ("sbuf", [128, 128], "int32"),
+    "lf": ("sbuf", [128, 128], "float32"),
+    "lw": ("sbuf", [128, 2048], "float32"),
+    "pl": ("sbuf", [128, 12, 16], "int32"),
+    "Z": ("sbuf", [128, 12, 32], "int32"),
+    "ZT": ("sbuf", [128, 384], "int32"),
+    "lu": ("sbuf", [128, 384], "uint16"),
+    "W": ("sbuf", [128, 6160], "bfloat16"),
     "x": ("sbuf", [128, 32], "int32"),
     "offi": ("sbuf", [128, 32], "int32"),
-    "offu": ("sbuf", [128, 32], "uint16"),
-    "xs": ("sbuf", [128, 32], "float32"),
-    "G": ("sbuf", [128, 512], "float32"),
-    "TT": ("sbuf", [128, 512], "float32"),
-    "m": ("sbuf", [128, 32], "float32"),
+    "offs": ("sbuf", [128, 96], "uint16"),
+    "rs": ("sbuf", [128, 4, 96], "uint16"),
+    "lst": ("sbuf", [128, 96], "uint16"),
+    "SY": ("sbuf", [128, 1536], "float32"),
+    "hi": ("sbuf", [128, 32], "int32"),
+    "sw": ("sbuf", [128, 64], "float32"),
+    "G": ("sbuf", [128, 512], "int32"),
+    "TT": ("sbuf", [128, 512], "int32"),
+    "Gf": ("sbuf", [128, 512], "float32"),
+    "Tf": ("sbuf", [128, 512], "float32"),
+    "fm": ("sbuf", [128, 32], "int32"),
+    "nn": ("sbuf", [128, 32], "float32"),
+    "mm": ("sbuf", [128, 32], "float32"),
     "x1": ("sbuf", [128, 32], "float32"),
     "F": ("sbuf", [128, 32], "bfloat16"),
-    "ir": ("sbuf", [128, 4, 104], "bfloat16"),
+    "ir": ("sbuf", [128, 104], "bfloat16"),
     "tm": ("sbuf", [128, 32], "float32"),
     "pa": ("sbuf", [128, 32], "float32"),
-    "pb": ("sbuf", [128, 32], "float32"),
     "posu": ("sbuf", [128, 32], "uint16"),
     "G2": ("sbuf", [128, 512], "bfloat16"),
     "T2": ("sbuf", [128, 512], "bfloat16"),
-    "pl": ("sbuf", [128, 3, 2, 4, 16], "int32"),
-    "Z": ("sbuf", [128, 4, 32], "float32"),
-    "ZT": ("sbuf", [128, 128], "float32"),
-    "lu": ("sbuf", [128, 384], "uint16"),
-    "W": ("sbuf", [128, 6160], "bfloat16"),
-    "syt": ("sbuf", [128, 96], "float32"),
     "xl": ("sbuf", [128, 32], "float32"),
     "xlt": ("sbuf", [128, 32], "float32"),
+    "rF": ("sbuf", [128, 4, 32], "float32"),
+    "zf": ("sbuf", [128, 512], "float32"),
     "onesf": ("sbuf", [128, 128], "float32"),
     "onesb": ("sbuf", [128, 128], "bfloat16"),
-    "e8": ("sbuf", [128, 128], "bfloat16"),
-    "zb": ("sbuf", [128, 512], "bfloat16"),
+    "zb": ("sbuf", [128, 32], "bfloat16"),
     "P0": ("sbuf", [128, 128], "float32"),
     "P1": ("sbuf", [128, 128], "float32"),
     "P2": ("sbuf", [128, 128], "float32"),
     "P3": ("sbuf", [128, 128], "float32"),
     "blk": ("sbuf", [128, 128], "bfloat16"),
-    "blk2": ("sbuf", [128, 128], "bfloat16"),
-    "A1": ("sbuf", [128, 128], "bfloat16"),
-    "A2": ("sbuf", [128, 128], "bfloat16"),
     "A3": ("sbuf", [128, 128], "bfloat16"),
-    "A4": ("sbuf", [128, 128], "bfloat16"),
+    "I1": ("sbuf", [128, 128], "bfloat16"),
     "E8": ("sbuf", [128, 128], "bfloat16"),
     "pxs": ("psum", [128, 512], "float32"),
     "pp": ("psum", [128, 512], "float32"),
     "ppos": ("psum", [128, 512], "float32"),
 }
-NDMA = 48
-SEMAPHORES = (["sv", "ss", "sp", "sg", "loc"] + ["d%d" % i for i in range(NDMA)] + ["ak%d" % r for r in range(N)]
-              + ["ai%d_%d" % (r, s) for r in range(N) for s in range(S)])
+NDMA = 70
+SEMAPHORES = (["sv", "ss", "sp", "sg", "loc"] + ["d%d" % i for i in range(NDMA)]
+              + ["%s%d" % (k, r) for k in ("ab", "aa", "ax", "au", "av", "af") for r in range(N)])
 
-VM = 14
 VB = 16
-VO = 48
+VO = 12
+WG = 768
 
 
 def rank_program(g, core, T, topo):
@@ -146,209 +152,254 @@ def rank_program(g, core, T, topo):
     def scopy(out, in_, reads, writes, deps=(), scale=1.0):
         return E("s", lambda: g.scalar.activation(out, in_, COPY, scale=scale), reads, writes, deps)
 
+    def mat(out, lhsT, rhs, start, stop, reads, writes):
+        return E("p", lambda: g.tensor.matmul(out, lhsT, rhs, start, stop), reads, writes)
+
     cores = list(T.cores)
 
-    def hops(r):
-        a, b = topo.chip(core), topo.chip(cores[r])
+    def hops(a, b):
+        a, b = topo.chip(cores[a]), topo.chip(cores[b])
         return 0 if a == b else (1 if topo.mates(a, b) or topo.same_plane(a, b) else 2)
 
-    near = sorted([r for r in range(N) if r != me], key=hops)
-    far = near[::-1]
-    engs = [e for e in topo.engines(core, cores[far[0]]) if all(e in topo.engines(core, cores[r]) for r in far)]
-    emask = 0
-    for e in engs:
-        emask |= 1 << e
-    ne = len(engs)
-    sent = [0]
+    def far_of(r):
+        return sorted([k for k in range(N) if k != r], key=lambda k: -hops(r, k))
 
-    def send(src, dst, sem):
-        ids = []
-        for r in far:
-            ad = topo.addr(cores[r])
-            ids.append(DstId(rid=ad[0], pnc=ad[1]))
-        g.remote_dma_fused([RemoteDMATransfer(dst_ids=ids, dma_engine_mask=emask, remote_sem=T.sem[sem],
-                                              srcs=[src], dsts=[dst for r in far])], local_sem=T.sem.loc)
+    def common(r):
+        f = far_of(r)
+        return [e for e in topo.engines(cores[r], cores[f[0]])
+                if all(e in topo.engines(cores[r], cores[k]) for k in f)]
+
+    def shares(r, turn):
+        e, f = common(r), far_of(r)
+        k = len(e) // 4
+        e = e[2 * k * turn:] + e[:2 * k * turn]
+        return {f[0]: e[0:2 * k], f[1]: e[2 * k:3 * k], f[2]: e[3 * k:4 * k]}
+
+    def bits(es):
+        m = 0
+        for e in es:
+            m |= 1 << e
+        return m
+
+    def dst(r):
+        ad = topo.addr(cores[r])
+        return DstId(rid=ad[0], pnc=ad[1])
+
+    far = far_of(me)
+    near = far[::-1]
+    ne = len(common(me))
+    sent = [0]
+    TURN = {"ab": 0, "ax": 1, "aa": 1}
+
+    def scatter(src, out, sem, reads):
+        for nm in reads:
+            need("g", wrote[nm][0])
+        sh = shares(me, TURN[sem])
+        g.remote_dma_fused([RemoteDMATransfer(dst_ids=[dst(r)], dma_engine_mask=bits(sh[r]),
+                                              remote_sem=T.sem["%s%d" % (sem, me)], srcs=[src[r]], dsts=[out[me]])
+                            for r in far], local_sem=T.sem.loc)
+        sent[0] += sum([len(sh[r]) for r in far])
+
+    def spread(src, out, sem, reads):
+        for nm in reads:
+            need("g", wrote[nm][0])
+        g.remote_dma_fused([RemoteDMATransfer(dst_ids=[dst(r) for r in far], dma_engine_mask=bits(common(me)),
+                                              remote_sem=T.sem[sem], srcs=[src], dsts=[out for r in far])],
+                           local_sem=T.sem.loc)
         sent[0] += ne
 
-    D("y", T.stin[:], T.stock[:], (), ["stin"])
-    for h in range(2):
-        D("s", T.mi[:, h, :], T.models[h::2, :], (), ["mi%d" % h])
-    for h in range(2):
-        D("y", T.si[h::2, :], T.states[h::2, :], (), ["si%d" % h])
-    for h in range(2):
-        D("y", T.le[:, h, :], T.letters[h::2, :], (), ["le%d" % h])
+    D("y", T.tx2[:], T.models[:], (), ["tx2"])
+    D("s", T.stin[:], T.stock[:], (), ["stin"])
+    D("y", T.tx0[:], T.states[:], (), ["tx0"])
+    for a in range(4):
+        D("y", T.pl[32 * a:32 * a + 32], T.places[2 * me + a // 2:2 * me + a // 2 + 1, :], (), ["pl%d" % a])
+    own2 = D("y", T.rx2[me], T.models[2 * me:2 * me + 2, :], (), ["own2"])
+    own0 = D("y", T.rx0[me], T.states[2 * me:2 * me + 2, :], (), ["own0"])
+    D("y", T.li[:], T.letters[:], (), ["li"])
 
-    def load_places(B):
-        for w in range(2):
-            D("y", T.pl[:, B, w], T.places[w::2, 2048 * B:2048 * B + 2048], (), ["pl%d_%d" % (B, w)])
-
-    load_places(0)
-
+    fw = [E("g", lambda: g.iota(T.win[:, 0:WG], [[1, WG]], 0, 0), (), ["wi"])]
+    vfill(T.zf[:], 0.0, "zf")
     vfill(T.onesf[:], 1.0, "onesf")
-    f0 = vfill(T.win[:, 0:512], 0.0, "wa")
     vfill(T.onesb[:], 1.0, "onesb")
-    vfill(T.e8[:], 8192.0, "e8")
-    vfill(T.zb[:], 0.0, "zb")
-    E("g", lambda: g.iota(T.sl[:], [[1, 64]], 0, 64), (), ["sl"])
+    vfill(T.blk[:], 0.0, "blk")
+    for t in range(2):
+        vfill(T.blk[64 * t:64 * t + 64, 64 * t:64 * t + 64], 1.0, "blk")
+    fw.append(vfill(T.win[:, WG:WG + 256], 0, "wa"))
+    fs, fl = [], []
+    for k in range(8):
+        fs.append(scopy(T.stw[:, 2048 + 512 * k:2560 + 512 * k], T.zf[:], ["zf"], ["sB%d" % k]))
+    for k in range(4):
+        fl.append(scopy(T.lw[:, 512 * k:512 * k + 512], T.zf[:], ["zf"], ["lz%d" % k]))
+
+    vcopy(T.stb[:], T.stin[:], ["stin"], ["stb"])
+    D("y", T.tx1[:], T.stb[:], ["stb"], ["tx1"])
+    own1 = D("y", T.rx1[me], T.stb[32 * me:32 * me + 32, :], ["stb"], ["own1"])
+
+    scatter([T.tx2[r] for r in range(N)], T.rx2, "ab", ["tx2"])
+    scatter([T.tx0[r] for r in range(N)], T.rx0, "ax", ["tx0"])
+    scatter([T.tx1[r] for r in range(N)], T.rx1, "aa", ["tx1"])
+
     for k, base in enumerate((0, -1000, -16, -1016)):
         out = T["P%d" % k]
         E("g", lambda: g.affine_select(out[:], T.onesf[:], [[-32, 4], [1000, 2], [-1, 16]], A.is_equal, 0.0, base, 1),
           ["onesf"], ["P%d" % k])
-    fw = [f0]
-    for k in range(3):
-        fw.append(scopy(T.win[:, 2560 + 512 * k:3072 + 512 * k], T.win[:, 0:512], ["wa"], ["wc%d" % k]))
-    fw.append(vfill(T.win[:, 512:2560], 0.0, "wb"))
-    vfill(T.ir[:, :, 0:8], 0.0, "irz")
+        if k == 0:
+            E("g", lambda: g.iota(T.sl[:], [[1, 128]], 0, 128), (), ["sl"])
+    ge = E("g", lambda: g.affine_select(T.I1[:], T.onesb[:], [[-1, 128]], A.is_equal, 0.0, 0, 1), ["onesb"], ["I1"])
+    for a in range(4):
+        ge = E("g", lambda: g.affine_select(T.A3[32 * a:32 * a + 32, :], T.blk[32 * a:32 * a + 32, :],
+                                            [[0, 2], [1, 2], [2, 32]], A.is_gt, 0.0, -(a % 2), -2),
+               ["blk"], ["A3_%d" % a], [ge])
+    A3 = ["A3_%d" % a for a in range(4)]
+
+    fw.append(vfill(T.win[:, WG + 256:2048], 0, "wb"))
+    fs.append(vfill(T.stw[:, 0:2048], 0.0, "sA"))
+    vfill(T.zb[:], 0.0, "zb")
+    vfill(T.ir[:, 0:8], 0.0, "irz")
     vfill(T.W[:, 0:16], 0.0, "wz")
-
-    vts(T.stb[:], T.stin[:], 2.0, A.mult, ["stin"], ["stb"])
-    need("g", wrote["stb"][0])
-    send(T.stb[:], T.stk[me], "ak%d" % me)
-
-    E("g", lambda: g.affine_select(T.blk[:], T.onesb[:], [[-16, 8], [0, 16]], A.is_ge, 0.0, 0, 1), ["onesb"], ["blk"])
-    E("g", lambda: g.affine_select(T.blk2[:], T.blk[:], [[16, 8], [0, 16]], A.is_ge, 0.0, 15, -1), ["blk"], ["blk2"])
-    E("g", lambda: g.affine_select(T.A3[:], T.blk2[:], [[1, 128]], A.is_gt, 0.0, 0, -1), ["blk2"], ["A3"])
-    E("g", lambda: g.affine_select(T.A4[:], T.blk2[:], [[-1, 128]], A.is_ge, 0.0, 0, 1), ["blk2"], ["A4"])
-    E("g", lambda: g.affine_select(T.E8[:], T.e8[:], [[-1, 128]], A.is_equal, 0.0, 0, 1), ["e8"], ["E8"])
-    if me > 0:
-        E("g", lambda: g.affine_select(T.A1[:], T.blk2[:], [[1, 128]], A.is_ge, 0.0, 0, -1), ["blk2"], ["A1"])
-        E("g", lambda: g.affine_select(T.A2[:], T.blk2[:], [[-1, 128]], A.is_gt, 0.0, 0, 1), ["blk2"], ["A2"])
-
+    for w in range(2):
+        vcopy(T.Z[:, :, 16 * w:16 * w + 16], T.pl[:], ["pl%d" % a for a in range(4)], ["Z%d" % w])
+    for u in range(12):
+        vtr(T.ZT[:, u::12], T.Z[:, u, :], ["Z0", "Z1"], ["ZT%d" % u])
+    vcopy(T.lu[:], T.ZT[:], ["ZT%d" % u for u in range(12)], ["lu"])
+    vcopy(T.lf[:], T.li[:], ["li"], ["lf"])
     vts(T.slm[:], T.sl[:], 2047, A.bitwise_and, ["sl"], ["slm"])
+
+    arr = {"ab": [own2], "ax": [own0], "aa": [own1]}
+    for r in near:
+        for nm in arr:
+            n = len(shares(r, TURN[nm])[me])
+            count["%s%d" % (nm, r)] = n
+            arr[nm].append(("%s%d" % (nm, r), n, "r"))
+    wd, sd = [], []
+    for t in range(2):
+        D("y", T.mi[64 * t:64 * t + 64, :], T.rx2[:, 64 * t:64 * t + 64, :], (), ["mi%d" % t], arr["ab"])
+    for t in range(2):
+        wd.append(D("y", T.win[64 * t:64 * t + 64:16, :], T.rx2[:, 64 * t:64 * t + 64, :], (), (), fw + arr["ab"]))
+    for t in range(2):
+        for w in range(2):
+            D("y", T.sx[64 * t:64 * t + 64, 16 * w:16 * w + 16], T.rx0[w::2, 64 * t:64 * t + 64, :],
+              (), ["sx%d%d" % (t, w)], arr["ax"])
+    for u in range(4):
+        for t in range(2):
+            p = 64 * t + 16 * u
+            sd.append(D("y", T.stw[p:p + 1, :], T.rx1[:, 64 * t:64 * t + 64, :], (), (), fs + arr["aa"]))
+    scopy(T.E8[:], T.I1[:], ["I1"], ["E8"], (), 8192.0)
+
     vts(T.mc[:], T.mi[:], 2047, A.bitwise_and, ["mi0", "mi1"], ["mc"])
     vts(T.mf[:], T.mi[:], 11, A.logical_shift_right, ["mi0", "mi1"], ["mf"])
-    for h in range(2):
-        vtt(T.qd[:, :, h], T.slm[:], T.mc[:, h, :], A.subtract, ["slm", "mc"], ["qd%d" % h])
-    for h in range(2):
-        vts(T.qf[:, :, h], T.mf[:, h, :], 1.0, A.add, ["mf"], ["qf%d" % h], (), 1.0 / 4096, A.mult)
-    wd = []
-    for k, nm in ((1, "qd"), (0, "qf")):
-        for w in range(2):
-            wd.append(D("y", T.win[16 * w + k::32, :], T[nm][:], [nm + "0", nm + "1"], (), fw))
-    for h in range(2):
-        vcopy(T.ql[:, :, h], T.le[:, h, :], ["le%d" % h], ["ql%d" % h])
-    for w in range(2):
-        wd.append(D("y", T.win[16 * w + 2::32, :], T.ql[:], ["ql0", "ql1"], (), fw))
+    vtt(T.qd[:], T.slm[:], T.mc[:], A.subtract, ["slm", "mc"], ["qd"])
+    vts(T.qf[:], T.mf[:], 1.0, A.add, ["mf"], ["qf"], (), 1.0 / 2048, A.mult)
+    lwd = [D("y", T.lw[k::16, :], T[nm][:], [nm], (), fl) for k, nm in ((1, "qd"), (0, "qf"), (2, "lf"))]
 
-    vcopy(T.sf[:], T.si[:], ["si0", "si1"], ["sf"])
-    vtr(T.sx[:], T.sf[:], ["sf"], ["sx"])
-    for h in range(2):
-        vts(T.x[:, h::2], T.sx[:, h::2], 2.0, A.mult, ["sx"], ["x%d" % h], (), float(h), A.add)
-    vts(T.hi[:, 0:1], T.sl[:, 0:1], 10, A.logical_shift_right, ["sl"], ["hi"], (), 1, A.bitwise_and)
-    vcopy(T.hf[:, 0:1], T.hi[:, 0:1], ["hi"], ["hf"])
-
-    def swap(out, w, src, r):
+    def swap(out, w, src, r, n):
         for c in range(2):
             for i in range(2):
-                E("p", lambda: g.tensor.matmul(out[:, c:32:2], T["P%d" % (2 * c + i)][:] if False else T["P%d" % (2 * c if False else (c * 2 + i))][:],
-                                               src[:, i:32:2], i == 0, i == 1),
-                  [r] + ["P%d" % (c * 2 + i)], [w])
-
-    def start_lookup():
-        vts(T.offi[:], T.x[:], 4095, A.bitwise_and, ["x0", "x1"], ["offi"])
-        vcopy(T.offu[:], T.offi[:], ["offi"], ["offu"])
-
-    def keep_high():
-        vtt(T.xs[:], T.x[:], T.offi[:], A.subtract, ["x0", "x1", "offi"], ["xs"])
-        swap(T.pxs, "pxs", T.xs, "xs")
-
-    start_lookup()
-    keep_high()
-
-    fs = [vfill(T.stw[:, 0:4096], 0.0, "stA")]
-    for k in range(4):
-        fs.append(scopy(T.stw[:, 4096 + 512 * k:4608 + 512 * k], T.zb[:], ["zb"], ["stB%d" % k]))
-    sd = [D("y", T.stw[0::16, Q * me:Q * me + Q], T.stb[:], ["stb"], (), fs)]
-    load_places(1)
-    load_places(2)
-    for r in near:
-        count["ak%d" % r] = ne
-        sd.append(D("y", T.stw[0::16, Q * r:Q * r + Q], T.stk[r], (), (), fs + [("ak%d" % r, ne, "r")]))
-
-    def list_of(B):
-        for w in range(2):
-            vcopy(T.Z[:, :, 16 * w:16 * w + 16], T.pl[:, B, w], ["pl%d_%d" % (B, w)], ["Z%d" % w])
-        for u in range(4):
-            vtr(T.ZT[:, u::4], T.Z[:, u, :], ["Z0", "Z1"], ["ZT%d" % u])
-        vcopy(T.lu[:, 128 * B:128 * B + 128], T.ZT[:], ["ZT%d" % u for u in range(4)], ["lu%d" % B])
+                nm = "P%d" % (2 * c + i)
+                mat(out[:, c:n:2], T[nm][:], src[:, i:n:2], i == 0, i == 1, r + [nm], [w])
 
     def order(B):
         w0, c0 = 16 + 2048 * B, 128 * B
-        scopy(T.W[:, w0 + 16 * VO:w0 + 2048], T.stw[:, 0:6144].indirect(T.lu[:, c0 + VO:c0 + 128]),
-              ["lu%d" % B], ["WS%d" % B], sd)
-        vcopy(T.W[:, w0:w0 + 16 * VO], T.stw[:, 0:6144].indirect(T.lu[:, c0:c0 + VO]),
-              ["lu%d" % B], ["WV%d" % B], sd)
+        k = VO if B == 0 else 0
+        scopy(T.W[:, w0 + 16 * k:w0 + 2048], T.stw[:, 0:6144].indirect(T.lu[:, c0 + k:c0 + 128]),
+              ["lu"], ["W%d" % B], sd)
+
+    def landed(nm, evs, d):
+        if d == me:
+            return [wrote[e][0] for e in evs]
+        count["%s%d" % (nm, d)] = ne
+        return [("%s%d" % (nm, d), ne, "r")]
+
+    def lists(c, e, nm, evs):
+        names = []
+        for d in [me] + near:
+            dep = landed(nm, evs, d)
+            for t in range(2):
+                p, o = 64 * t + 16 * me, 32 * d + 16 * t
+                names.append("l%s%d_%d" % (nm, d, t))
+                D("y", T.lst[o:o + 16, c:e], T.offs[p:p + 16, c:e] if d == me else T.rs[p:p + 16, d, c:e],
+                  (), [names[-1]], dep)
+        return names
+
+    vtr(T.x[:], T.sx[:], ["sx00", "sx01", "sx10", "sx11"], ["x"])
+    order(0)
 
     for s in range(S):
         last = s == S - 1
-        if s > 0:
-            start_lookup()
-        scopy(T.G[:, 16 * VM:512], T.win[:, 0:4096].indirect(T.offu[:, VM:32]), ["offu"], ["GS"], wd)
-        if s > 0:
-            keep_high()
-        vcopy(T.G[:, 0:16 * VM], T.win[:, 0:4096].indirect(T.offu[:, 0:VM]), ["offu"], ["GV"], wd)
-        vtr(T.TT[:, 0:16 * VM], T.G[:, 0:16 * VM], ["GV"], ["TV"])
-        vtr(T.TT[:, 16 * VM:512], T.G[:, 16 * VM:512], ["GS"], ["TS"])
-        vtt(T.m[:], T.TT[:, 0::16], T.pxs[:, 0:32], A.mult, ["TV", "TS", "pxs"], ["m"])
-        vtt(T.x1[:], T.m[:], T.TT[:, 1::16], A.add, ["m", "TV", "TS"], ["xn"])
-        vts(T.F[:], T.x1[:], 4096.0, A.is_lt, ["xn"], ["F"])
-        c0 = 8 + 32 * s
-        prev = "irz" if s == 0 else "ir%d_%d" % (me, s - 1)
-        E("v", lambda: V.tensor_tensor_scan(T.ir[:, me, c0:c0 + 32], T.F[:], T.zb[:, 0:32],
-                                            T.ir[:, me, c0 - 1:c0], A.add, A.add),
-          ["F", "zb", prev], ["ir%d_%d" % (me, s)])
-        need("g", wrote["ir%d_%d" % (me, s)][0])
-        send(T.ir[:, me, c0:c0 + 32], T.ir[:, me, c0:c0 + 32], "ai%d_%d" % (me, s))
-
-        def count_in(r, first, final):
-            hi, lo = ("A1", "A2") if r < me else ("A3", "A4")
-            rd = ["ir%d_%d" % (r, s), "irz"] + ([] if s == 0 else ["ir%d_%d" % (r, s - 1)])
-            E("p", lambda: g.tensor.matmul(T.ppos[:, 0:32], T[hi][:], T.ir[:, r, c0:c0 + 32], first, False),
-              rd + [hi], ["ppos"])
-            E("p", lambda: g.tensor.matmul(T.ppos[:, 0:32], T[lo][:], T.ir[:, r, c0 - 1:c0 + 31], False, final),
-              rd + [lo], ["ppos"])
-
-        count_in(me, True, False)
-        E("p", lambda: g.tensor.matmul(T.ppos[:, 0:32], T.E8[:], T.F[:], False, False), ["F", "E8"], ["ppos"])
-
+        slots = "of%d" % s
+        off = T.offs[:, 32 * s:32 * s + 32]
+        vts(T.offi[:], T.x[:], 2047, A.bitwise_and, ["x"], ["offi"])
+        vcopy(off, T.offi[:], ["offi"], [slots])
         if s == 0:
-            list_of(0)
-        vts(T.tm[:], T.F[:], 255.0 if last else 510.0, A.mult, ["F"], ["tm"], (), 1.0 if last else 2.0, A.add)
-        vtt(T.pa[:], T.x1[:], T.tm[:], A.mult, ["xn", "tm"], ["pa"])
-        if last:
-            swap(T.pp, "pp", T.pa, "pa")
+            vts(T.hi[:], T.x[:], 11, A.logical_shift_right, ["x"], ["hi"])
+            vts(T.sw[:, 0:32], T.hi[:], 2048.0, A.add, ["hi"], ["sw"])
+            vtt(T.sw[:, 32:64], T.hi[:], T.offi[:], A.add, ["hi", "offi"], ["swb"])
+            swap(T.pxs, "pxs", T.sw, ["sw", "swb"], 64)
+            vcopy(T.G[:], T.win[:, 0:2048].indirect(off), [slots], ["G"], wd)
+            vtr(T.TT[:], T.G[:], ["G"], ["TT"])
+            vts(T.fm[:], T.TT[:, 0::16], 11, A.logical_shift_right, ["TT"], ["fm"])
+            vtt(T.nn[:], T.pxs[:, 32:64], T.TT[:, 0::16], A.subtract, ["pxs", "TT"], ["nn"])
+            vtt(T.mm[:], T.fm[:], T.pxs[:, 0:32], A.mult, ["fm", "pxs"], ["mm"])
+            vtt(T.x1[:], T.mm[:], T.nn[:], A.add, ["mm", "nn"], ["x1"])
         else:
-            vts(T.pb[:], T.pa[:], T.hf[:, 0:1], A.add, ["pa", "hf"], ["pb"])
-            swap(T.pp, "pp", T.pb, "pb")
-        vtr(T.syt[:, 32 * s:32 * s + 32], T.TT[:, 2::16], ["TV", "TS"], ["sy%d" % s])
-        order(s)
-        for w in range(2):
-            D("y", T.syms[w::2, 512 * s:512 * s + 512], T.syt[:, 32 * s + 16 * w:32 * s + 16 * w + 16], ["sy%d" % s])
-        if not last:
-            list_of(s + 1)
+            vtt(T.sw[:, 0:32], T.x[:], T.offi[:], A.subtract, ["x", "offi"], ["sw"])
+            swap(T.pxs, "pxs", T.sw, ["sw"], 32)
+            vcopy(T.Gf[:], T.lw[:, 0:2048].indirect(off), [slots], ["Gf"], lwd)
+            if s == 1:
+                spread(T.offs[:, 0:64], T.rs[:, me, 0:64], "au%d" % me, ["of0", "of1"])
+            else:
+                spread(T.offs[:, 64:96], T.rs[:, me, 64:96], "av%d" % me, ["of2"])
+            vtr(T.Tf[:], T.Gf[:], ["Gf"], ["Tf"])
+            vtt(T.mm[:], T.Tf[:, 0::16], T.pxs[:, 0:32], A.mult, ["Tf", "pxs"], ["mm"])
+            vtt(T.x1[:], T.mm[:], T.Tf[:, 1::16], A.add, ["mm", "Tf"], ["x1"])
+        vts(T.F[:], T.x1[:], 4096.0, A.is_lt, ["x1"], ["F"])
+        c0 = 8 + 32 * s
+        prev = "irz" if s == 0 else "ir%d" % (s - 1)
+        E("v", lambda: V.tensor_tensor_scan(T.ir[:, c0:c0 + 32], T.F[:], T.zb[:], T.ir[:, c0 - 1:c0], A.add, A.add),
+          ["F", "zb", prev], ["ir%d" % s])
 
-        for i, r in enumerate(near):
-            nm = "ai%d_%d" % (r, s)
-            count[nm] = ne
-            wrote["ir%d_%d" % (r, s)] = [(nm, ne, "r")]
-            count_in(r, False, i == N - 2)
+        mat(T.ppos[:, 0:32], T.E8[:], T.F[:], True, False, ["F", "E8"], ["ppos"])
+        mat(T.ppos[:, 1:32:2], T.I1[:], T.F[:, 0:32:2], False, False, ["F", "I1"], ["ppos"])
+        for h in range(2):
+            for k in range(2):
+                mat(T.ppos[:, h:32:2], T.A3[:], T.F[:, k:32:2], False, False, ["F"] + A3, ["ppos"])
+        for h in range(2):
+            mat(T.ppos[:, h:32:2], T.blk[:], T.ir[:, c0 - 1:c0 + 31:2], False, h == 1, ["ir%d" % s, prev, "blk"],
+                ["ppos"])
+
+        vts(T.tm[:], T.F[:], 255.0, A.mult, ["F"], ["tm"], (), 1.0, A.add)
+        vtt(T.pa[:], T.x1[:], T.tm[:], A.mult, ["x1", "tm"], ["pa"])
+        swap(T.pp, "pp", T.pa, ["pa"], 32)
+        if s == 0:
+            vcopy(T.W[:, 16:16 + 16 * VO], T.stw[:, 0:6144].indirect(T.lu[:, 0:VO]), ["lu"], ["WV"], sd)
         vts(T.posu[:], T.ppos[:, 0:32], -8176.0, A.add, ["ppos"], ["posu"], (), 0.0, A.max)
-        wr = ["posu", "wz"] + ["WS%d" % B for B in range(s + 1)] + ["WV%d" % B for B in range(s + 1)]
+        wr = ["posu", "wz", "WV"] + ["W%d" % B for B in range(s + 1)]
         win2 = T.W[:, 0:16 + 2048 * (s + 1)]
-        scopy(T.G2[:, 16 * VB:512], win2.indirect(T.posu[:, VB:32]), wr, ["HS"], (), 0.5 if last else 1.0)
-        if last:
-            vts(T.G2[:, 0:16 * VB], win2.indirect(T.posu[:, 0:VB]), 0.5, A.mult, wr, ["HV"])
-        else:
-            vcopy(T.G2[:, 0:16 * VB], win2.indirect(T.posu[:, 0:VB]), wr, ["HV"])
-        vtr(T.T2[:, 0:16 * VB], T.G2[:, 0:16 * VB], ["HV"], ["UV"])
-        vtr(T.T2[:, 16 * VB:512], T.G2[:, 16 * VB:512], ["HS"], ["US"])
+        scopy(T.G2[:, 16 * VB:512], win2.indirect(T.posu[:, VB:32]), wr, ["HS"])
+        vcopy(T.G2[:, 0:16 * VB], win2.indirect(T.posu[:, 0:VB]), wr, ["HV"])
         if not last:
-            vtt(T.x[:], T.T2[:, 0::16], T.pp[:, 0:32], A.add, ["UV", "US", "pp"], ["x0", "x1"])
+            order(s + 1)
+        vtr(T.T2[:], T.G2[:], ["HV", "HS"], ["T2"])
+        if not last:
+            vtt(T.x[:], T.T2[:, 0::16], T.pp[:, 0:32], A.add, ["T2", "pp"], ["x"])
         else:
-            vtt(T.xl[:], T.T2[:, 0::16], T.pp[:, 0:32], A.add, ["UV", "US", "pp"], ["xl"])
+            vtt(T.xl[:], T.T2[:, 0::16], T.pp[:, 0:32], A.add, ["T2", "pp"], ["xl"])
             vtr(T.xlt[:], T.xl[:], ["xl"], ["xlt"])
-            for h, q in ((0, "y"), (1, "s")):
-                D(q, T.last[h::2, :], T.xlt[h::2, :], ["xlt"])
+            spread(T.xlt[:], T.rF[:, me, :], "af%d" % me, ["xlt"])
+
+    lu01 = lists(0, 64, "au", ["of0", "of1"])
+    lu2 = lists(64, 96, "av", ["of2"])
+    scopy(T.SY[:, 0:2 * L], T.lw[:, 0:2048].indirect(T.lst[:, 0:64]), lu01, ["sy01"], lwd)
+    vcopy(T.SY[:, 2 * L:3 * L], T.lw[:, 0:2048].indirect(T.lst[:, 64:96]), lu2, ["sy2"], lwd)
+    D("s", T.syms[:, 0:2 * L], T.SY[2::16, 0:2 * L], ["sy01"])
+    D("y", T.syms[:, 2 * L:3 * L], T.SY[2::16, 2 * L:3 * L], ["sy2"])
+    i, w = me // 2, me % 2
+    for d in [me] + near:
+        dep = landed("af", ["xlt"], d)
+        for t, q in ((0, "y"), (1, "s")):
+            p = 64 * t + 32 * i
+            xs = T.xlt[p:p + 32, 16 * w:16 * w + 16] if d == me else T.rF[p:p + 32, d, 16 * w:16 * w + 16]
+            D(q, T.last[2 * d + t:2 * d + t + 1, :], xs, (), (), dep)
 
     for sem in sorted(count):
         if max([known.get((q, sem), 0) for q in queues]) < count[sem]:

@@ -21,13 +21,19 @@ SCRATCH = {
     "slm": ("sbuf", [128, 128], "int32"),
     "qf": ("sbuf", [128, 128], "float32"),
     "qd": ("sbuf", [128, 128], "float32"),
+    "qe": ("sbuf", [128, 128], "float32"),
     "li": ("sbuf", [128, 128], "int32"),
     "lf": ("sbuf", [128, 128], "float32"),
     "lw": ("sbuf", [128, 2048], "float32"),
-    "pl": ("sbuf", [128, 12, 16], "int32"),
-    "Z": ("sbuf", [128, 12, 32], "int32"),
-    "ZT": ("sbuf", [128, 384], "int32"),
-    "lu": ("sbuf", [128, 384], "uint16"),
+    "pl": ("sbuf", [128, 4, 16], "int32"),
+    "pk": ("sbuf", [128, 64], "int32"),
+    "Z": ("sbuf", [128, 4, 32], "int32"),
+    "ZT": ("sbuf", [128, 128], "int32"),
+    "ZK": ("sbuf", [128, 64], "int32"),
+    "lu": ("sbuf", [128, 128], "uint16"),
+    "lk": ("sbuf", [128, 64], "uint16"),
+    "R1": ("sbuf", [128, 512], "bfloat16"),
+    "R2": ("sbuf", [128, 512], "bfloat16"),
     "W": ("sbuf", [128, 6160], "bfloat16"),
     "x": ("sbuf", [128, 32], "int32"),
     "offi": ("sbuf", [128, 32], "int32"),
@@ -36,6 +42,8 @@ SCRATCH = {
     "lst": ("sbuf", [128, 96], "uint16"),
     "SY": ("sbuf", [128, 1536], "float32"),
     "hi": ("sbuf", [128, 32], "int32"),
+    "pai": ("sbuf", [128, 32], "int32"),
+    "hb": ("sbuf", [128, 32], "int32"),
     "sw": ("sbuf", [128, 64], "float32"),
     "G": ("sbuf", [128, 512], "int32"),
     "TT": ("sbuf", [128, 512], "int32"),
@@ -46,7 +54,7 @@ SCRATCH = {
     "mm": ("sbuf", [128, 32], "float32"),
     "x1": ("sbuf", [128, 32], "float32"),
     "F": ("sbuf", [128, 32], "bfloat16"),
-    "ir": ("sbuf", [128, 104], "bfloat16"),
+    "ir": ("sbuf", [128, 128], "bfloat16"),
     "tm": ("sbuf", [128, 32], "float32"),
     "pa": ("sbuf", [128, 32], "float32"),
     "posu": ("sbuf", [128, 32], "uint16"),
@@ -55,28 +63,27 @@ SCRATCH = {
     "xl": ("sbuf", [128, 32], "float32"),
     "xlt": ("sbuf", [128, 32], "float32"),
     "rF": ("sbuf", [128, 4, 32], "float32"),
-    "zf": ("sbuf", [128, 512], "float32"),
     "onesf": ("sbuf", [128, 128], "float32"),
-    "onesb": ("sbuf", [128, 128], "bfloat16"),
-    "zb": ("sbuf", [128, 32], "bfloat16"),
     "P0": ("sbuf", [128, 128], "float32"),
     "P1": ("sbuf", [128, 128], "float32"),
     "P2": ("sbuf", [128, 128], "float32"),
     "P3": ("sbuf", [128, 128], "float32"),
     "blk": ("sbuf", [128, 128], "bfloat16"),
     "A3": ("sbuf", [128, 128], "bfloat16"),
-    "I1": ("sbuf", [128, 128], "bfloat16"),
-    "E8": ("sbuf", [128, 128], "bfloat16"),
+    "M1": ("sbuf", [128, 128], "bfloat16"),
+    "AI": ("sbuf", [128, 128], "bfloat16"),
     "pxs": ("psum", [128, 512], "float32"),
     "pp": ("psum", [128, 512], "float32"),
     "ppos": ("psum", [128, 512], "float32"),
 }
-NDMA = 70
+NDMA = 104
 SEMAPHORES = (["sv", "ss", "sp", "sg", "loc"] + ["d%d" % i for i in range(NDMA)]
-              + ["%s%d" % (k, r) for k in ("ab", "aa", "ax", "au", "av", "af") for r in range(N)])
+              + ["%s%d" % (k, r) for k in ("ab", "aa", "ax", "av", "af") for r in range(N)])
 
-VB = 16
-VO = 12
+VG = 16
+VB = 14
+VL = 16
+SF = 8
 WG = 768
 
 
@@ -149,8 +156,8 @@ def rank_program(g, core, T, topo):
     def vtr(out, in_, reads, writes):
         return E("v", lambda: V.transpose(out, in_), reads, writes)
 
-    def scopy(out, in_, reads, writes, deps=(), scale=1.0):
-        return E("s", lambda: g.scalar.activation(out, in_, COPY, scale=scale), reads, writes, deps)
+    def scopy(out, in_, reads, writes, deps=()):
+        return E("s", lambda: g.scalar.activation(out, in_, COPY), reads, writes, deps)
 
     def mat(out, lhsT, rhs, start, stop, reads, writes):
         return E("p", lambda: g.tensor.matmul(out, lhsT, rhs, start, stop), reads, writes)
@@ -208,35 +215,36 @@ def rank_program(g, core, T, topo):
                            local_sem=T.sem.loc)
         sent[0] += ne
 
+    D("y", T.tx0[:], T.states[:], (), ["tx0"])
     D("y", T.tx2[:], T.models[:], (), ["tx2"])
     D("s", T.stin[:], T.stock[:], (), ["stin"])
-    D("y", T.tx0[:], T.states[:], (), ["tx0"])
     for a in range(4):
-        D("y", T.pl[32 * a:32 * a + 32], T.places[2 * me + a // 2:2 * me + a // 2 + 1, :], (), ["pl%d" % a])
+        D("y", T.pl[32 * a:32 * a + 32], T.places[2 * me + a // 2:2 * me + a // 2 + 1, 0:2048], (), ["pl%d" % a])
     own2 = D("y", T.rx2[me], T.models[2 * me:2 * me + 2, :], (), ["own2"])
     own0 = D("y", T.rx0[me], T.states[2 * me:2 * me + 2, :], (), ["own0"])
     D("y", T.li[:], T.letters[:], (), ["li"])
 
     fw = [E("g", lambda: g.iota(T.win[:, 0:WG], [[1, WG]], 0, 0), (), ["wi"])]
-    vfill(T.zf[:], 0.0, "zf")
+    fs = [vfill(T.stw[:, 0:512], 0.0, "sA")]
     vfill(T.onesf[:], 1.0, "onesf")
-    vfill(T.onesb[:], 1.0, "onesb")
     vfill(T.blk[:], 0.0, "blk")
     for t in range(2):
         vfill(T.blk[64 * t:64 * t + 64, 64 * t:64 * t + 64], 1.0, "blk")
     fw.append(vfill(T.win[:, WG:WG + 256], 0, "wa"))
-    fs, fl = [], []
-    for k in range(8):
-        fs.append(scopy(T.stw[:, 2048 + 512 * k:2560 + 512 * k], T.zf[:], ["zf"], ["sB%d" % k]))
+    fl = []
+    for k in range(12 - SF, 12):
+        fs.append(scopy(T.stw[:, 512 * k:512 * k + 512], T.stw[:, 0:512], ["sA"], ["sB%d" % k]))
     for k in range(4):
-        fl.append(scopy(T.lw[:, 512 * k:512 * k + 512], T.zf[:], ["zf"], ["lz%d" % k]))
+        fl.append(scopy(T.lw[:, 512 * k:512 * k + 512], T.lw[:, 0:512] if k else T.stw[:, 0:512], ["lz0" if k else "sA"],
+                        ["lz%d" % k]))
+    fs.append(fl[0])
 
     vcopy(T.stb[:], T.stin[:], ["stin"], ["stb"])
     D("y", T.tx1[:], T.stb[:], ["stb"], ["tx1"])
     own1 = D("y", T.rx1[me], T.stb[32 * me:32 * me + 32, :], ["stb"], ["own1"])
 
-    scatter([T.tx2[r] for r in range(N)], T.rx2, "ab", ["tx2"])
     scatter([T.tx0[r] for r in range(N)], T.rx0, "ax", ["tx0"])
+    scatter([T.tx2[r] for r in range(N)], T.rx2, "ab", ["tx2"])
     scatter([T.tx1[r] for r in range(N)], T.rx1, "aa", ["tx1"])
 
     for k, base in enumerate((0, -1000, -16, -1016)):
@@ -245,24 +253,26 @@ def rank_program(g, core, T, topo):
           ["onesf"], ["P%d" % k])
         if k == 0:
             E("g", lambda: g.iota(T.sl[:], [[1, 128]], 0, 128), (), ["sl"])
-    ge = E("g", lambda: g.affine_select(T.I1[:], T.onesb[:], [[-1, 128]], A.is_equal, 0.0, 0, 1), ["onesb"], ["I1"])
     for a in range(4):
-        ge = E("g", lambda: g.affine_select(T.A3[32 * a:32 * a + 32, :], T.blk[32 * a:32 * a + 32, :],
-                                            [[0, 2], [1, 2], [2, 32]], A.is_gt, 0.0, -(a % 2), -2),
-               ["blk"], ["A3_%d" % a], [ge])
+        E("g", lambda: g.affine_select(T.A3[32 * a:32 * a + 32, :], T.blk[32 * a:32 * a + 32, :],
+                                       [[0, 2], [1, 2], [2, 32]], A.is_gt, 0.0, -(a % 2), -2), ["blk"], ["A3_%d" % a],
+          [("sg", count["sg"], "g")])
     A3 = ["A3_%d" % a for a in range(4)]
+    for nm, c in (("M1", 8192.0), ("AI", 1.0)):
+        E("g", lambda: g.affine_select(T[nm][:], T.A3[:], [[-1, 128]], A.not_equal, c, 0, 1), A3, [nm])
+    E("g", lambda: g.iota(T.W[:, 4112:6160], [[0, 2048]], 0, 0, allow_small_or_imprecise_dtypes=True), (), ["wz2"])
 
     fw.append(vfill(T.win[:, WG + 256:2048], 0, "wb"))
-    fs.append(vfill(T.stw[:, 0:2048], 0.0, "sA"))
-    vfill(T.zb[:], 0.0, "zb")
-    vfill(T.ir[:, 0:8], 0.0, "irz")
+    fs.append(vfill(T.stw[:, 512:6144 - 512 * SF], 0.0, "sC"))
+    vfill(T.ir[:, 0:32], 0.0, "irz")
     vfill(T.W[:, 0:16], 0.0, "wz")
     for w in range(2):
         vcopy(T.Z[:, :, 16 * w:16 * w + 16], T.pl[:], ["pl%d" % a for a in range(4)], ["Z%d" % w])
-    for u in range(12):
-        vtr(T.ZT[:, u::12], T.Z[:, u, :], ["Z0", "Z1"], ["ZT%d" % u])
-    vcopy(T.lu[:], T.ZT[:], ["ZT%d" % u for u in range(12)], ["lu"])
+    for u in range(4):
+        vtr(T.ZT[:, u::4], T.Z[:, u, :], ["Z0", "Z1"], ["ZT%d" % u])
+    vcopy(T.lu[:], T.ZT[:], ["ZT%d" % u for u in range(4)], ["lu"])
     vcopy(T.lf[:], T.li[:], ["li"], ["lf"])
+    vfill(T.W[:, 2064:4112], 0.0, "wz1")
     vts(T.slm[:], T.sl[:], 2047, A.bitwise_and, ["sl"], ["slm"])
 
     arr = {"ab": [own2], "ax": [own0], "aa": [own1]}
@@ -273,24 +283,31 @@ def rank_program(g, core, T, topo):
             arr[nm].append(("%s%d" % (nm, r), n, "r"))
     wd, sd = [], []
     for t in range(2):
-        D("y", T.mi[64 * t:64 * t + 64, :], T.rx2[:, 64 * t:64 * t + 64, :], (), ["mi%d" % t], arr["ab"])
-    for t in range(2):
-        wd.append(D("y", T.win[64 * t:64 * t + 64:16, :], T.rx2[:, 64 * t:64 * t + 64, :], (), (), fw + arr["ab"]))
-    for t in range(2):
         for w in range(2):
             D("y", T.sx[64 * t:64 * t + 64, 16 * w:16 * w + 16], T.rx0[w::2, 64 * t:64 * t + 64, :],
               (), ["sx%d%d" % (t, w)], arr["ax"])
+    for t in range(2):
+        wd.append(D("y", T.win[64 * t:64 * t + 64:16, :], T.rx2[:, 64 * t:64 * t + 64, :], (), (), fw + arr["ab"]))
     for u in range(4):
         for t in range(2):
             p = 64 * t + 16 * u
             sd.append(D("y", T.stw[p:p + 1, :], T.rx1[:, 64 * t:64 * t + 64, :], (), (), fs + arr["aa"]))
-    scopy(T.E8[:], T.I1[:], ["I1"], ["E8"], (), 8192.0)
+    for t in range(2):
+        D("y", T.mi[64 * t:64 * t + 64, :], T.rx2[:, 64 * t:64 * t + 64, :], (), ["mi%d" % t], arr["ab"])
 
-    vts(T.mc[:], T.mi[:], 2047, A.bitwise_and, ["mi0", "mi1"], ["mc"])
-    vts(T.mf[:], T.mi[:], 11, A.logical_shift_right, ["mi0", "mi1"], ["mf"])
-    vtt(T.qd[:], T.slm[:], T.mc[:], A.subtract, ["slm", "mc"], ["qd"])
-    vts(T.qf[:], T.mf[:], 1.0, A.add, ["mf"], ["qf"], (), 1.0 / 2048, A.mult)
-    lwd = [D("y", T.lw[k::16, :], T[nm][:], [nm], (), fl) for k, nm in ((1, "qd"), (0, "qf"), (2, "lf"))]
+    pk = []
+    for B in range(2):
+        for a in range(4):
+            for w in range(2):
+                o, c = 2048 * (B + 1) + 1024 * (a % 2) + 512 * w, 32 * B + 16 * w
+                pk.append("pk%d" % len(pk))
+                D("y", T.pk[32 * a:32 * a + 32, c:c + 16], T.places[2 * me + a // 2:2 * me + a // 2 + 1, o:o + 512],
+                  (), [pk[-1]])
+
+    lwd = [D("y", T.lw[2::16, :], T.lf[:], ["lf"], (), fl)]
+
+    def second(k, nm):
+        lwd.append(D("y", T.lw[k::16, :], T[nm][:], [nm], (), fl))
 
     def swap(out, w, src, r, n):
         for c in range(2):
@@ -299,70 +316,65 @@ def rank_program(g, core, T, topo):
                 mat(out[:, c:n:2], T[nm][:], src[:, i:n:2], i == 0, i == 1, r + [nm], [w])
 
     def order(B):
-        w0, c0 = 16 + 2048 * B, 128 * B
-        k = VO if B == 0 else 0
-        scopy(T.W[:, w0 + 16 * k:w0 + 2048], T.stw[:, 0:6144].indirect(T.lu[:, c0 + k:c0 + 128]),
-              ["lu"], ["W%d" % B], sd)
-
-    def landed(nm, evs, d):
-        if d == me:
-            return [wrote[e][0] for e in evs]
-        count["%s%d" % (nm, d)] = ne
-        return [("%s%d" % (nm, d), ne, "r")]
-
-    def lists(c, e, nm, evs):
-        names = []
-        for d in [me] + near:
-            dep = landed(nm, evs, d)
-            for t in range(2):
-                p, o = 64 * t + 16 * me, 32 * d + 16 * t
-                names.append("l%s%d_%d" % (nm, d, t))
-                D("y", T.lst[o:o + 16, c:e], T.offs[p:p + 16, c:e] if d == me else T.rs[p:p + 16, d, c:e],
-                  (), [names[-1]], dep)
-        return names
+        src = "R%d" % B
+        scopy(T[src][:], T.stw[:, 0:6144].indirect(T.lk[:, 32 * B - 32:32 * B]), ["lk"], [src], sd)
+        for t in range(2):
+            for u in range(4):
+                p = 64 * t + 16 * u
+                D("y", T.W[p:p + 1, 16 + 2048 * B:2064 + 2048 * B], T[src][64 * t:64 * t + 64:16, :], [src],
+                  ["W%d_%d" % (B, 4 * t + u)], wrote["wz%d" % B])
 
     vtr(T.x[:], T.sx[:], ["sx00", "sx01", "sx10", "sx11"], ["x"])
-    order(0)
-
+    scopy(T.W[:, 16:2064], T.stw[:, 0:6144].indirect(T.lu[:]), ["lu"], ["W0"], sd)
+    wr = ["posu", "wz", "W0"]
     for s in range(S):
         last = s == S - 1
         slots = "of%d" % s
-        off = T.offs[:, 32 * s:32 * s + 32]
+        o = 32 * s
         vts(T.offi[:], T.x[:], 2047, A.bitwise_and, ["x"], ["offi"])
-        vcopy(off, T.offi[:], ["offi"], [slots])
+        vcopy(T.offs[:, o:o + 32], T.offi[:], ["offi"], [slots])
         if s == 0:
             vts(T.hi[:], T.x[:], 11, A.logical_shift_right, ["x"], ["hi"])
             vts(T.sw[:, 0:32], T.hi[:], 2048.0, A.add, ["hi"], ["sw"])
             vtt(T.sw[:, 32:64], T.hi[:], T.offi[:], A.add, ["hi", "offi"], ["swb"])
             swap(T.pxs, "pxs", T.sw, ["sw", "swb"], 64)
-            vcopy(T.G[:], T.win[:, 0:2048].indirect(off), [slots], ["G"], wd)
+            vcopy(T.G[:], T.win[:, 0:2048].indirect(T.offs[:, o:o + 32]), [slots], ["G"], wd)
+            vts(T.mc[:], T.mi[:], 2047, A.bitwise_and, ["mi0", "mi1"], ["mc"])
             vtr(T.TT[:], T.G[:], ["G"], ["TT"])
+            vts(T.mf[:], T.mi[:], 11, A.logical_shift_right, ["mi0", "mi1"], ["mf"])
             vts(T.fm[:], T.TT[:, 0::16], 11, A.logical_shift_right, ["TT"], ["fm"])
             vtt(T.nn[:], T.pxs[:, 32:64], T.TT[:, 0::16], A.subtract, ["pxs", "TT"], ["nn"])
             vtt(T.mm[:], T.fm[:], T.pxs[:, 0:32], A.mult, ["fm", "pxs"], ["mm"])
+            vtt(T.qd[:], T.slm[:], T.mc[:], A.subtract, ["slm", "mc"], ["qd"])
+            second(1, "qd")
             vtt(T.x1[:], T.mm[:], T.nn[:], A.add, ["mm", "nn"], ["x1"])
+            vts(T.qf[:], T.mf[:], 1.0, A.add, ["mf"], ["qf"], (), 1.0 / 2048, A.mult)
+            second(0, "qf")
+            vts(T.F[:], T.x1[:], 4096.0, A.is_lt, ["x1"], ["F"])
         else:
-            vtt(T.sw[:, 0:32], T.x[:], T.offi[:], A.subtract, ["x", "offi"], ["sw"])
-            swap(T.pxs, "pxs", T.sw, ["sw"], 32)
-            vcopy(T.Gf[:], T.lw[:, 0:2048].indirect(off), [slots], ["Gf"], lwd)
-            if s == 1:
-                spread(T.offs[:, 0:64], T.rs[:, me, 0:64], "au%d" % me, ["of0", "of1"])
-            else:
-                spread(T.offs[:, 64:96], T.rs[:, me, 64:96], "av%d" % me, ["of2"])
-            vtr(T.Tf[:], T.Gf[:], ["Gf"], ["Tf"])
-            vtt(T.mm[:], T.Tf[:, 0::16], T.pxs[:, 0:32], A.mult, ["Tf", "pxs"], ["mm"])
+            lw = T.lw[:, 0:2048]
+            scopy(T.Gf[:, 16 * VG:512], lw.indirect(T.offs[:, o + VG:o + 32]), [slots], ["GS"], lwd)
+            if not last:
+                order(2)
+            vcopy(T.Gf[:, 0:16 * VG], lw.indirect(T.offs[:, o:o + VG]), [slots], ["GV"], lwd)
+            if last:
+                spread(T.offs[:], T.rs[:, me, :], "av%d" % me, ["of0", "of1", "of2"])
+            vtr(T.Tf[:], T.Gf[:], ["GV", "GS"], ["Tf"])
+            vtt(T.mm[:], T.Tf[:, 0::16], T.hb[:], A.mult, ["Tf", "hb"], ["mm"])
+            vtt(T.F[:], T.mm[:], T.Tf[:, 3::16], A.is_lt, ["mm", "Tf"], ["F"])
             vtt(T.x1[:], T.mm[:], T.Tf[:, 1::16], A.add, ["mm", "Tf"], ["x1"])
-        vts(T.F[:], T.x1[:], 4096.0, A.is_lt, ["x1"], ["F"])
-        c0 = 8 + 32 * s
+        c0 = 32 + 32 * s
         prev = "irz" if s == 0 else "ir%d" % (s - 1)
-        E("v", lambda: V.tensor_tensor_scan(T.ir[:, c0:c0 + 32], T.F[:], T.zb[:], T.ir[:, c0 - 1:c0], A.add, A.add),
-          ["F", "zb", prev], ["ir%d" % s])
+        E("v", lambda: V.tensor_tensor_scan(T.ir[:, c0:c0 + 32], T.F[:], T.ir[:, 0:32], T.ir[:, c0 - 1:c0], A.add, A.add),
+          ["F", "irz", prev], ["ir%d" % s])
+        if s == 0:
+            vts(T.qe[:], T.qd[:], -1.0, A.mult, ["qd"], ["qe"], (), 4096.0, A.add)
+            second(3, "qe")
 
-        mat(T.ppos[:, 0:32], T.E8[:], T.F[:], True, False, ["F", "E8"], ["ppos"])
-        mat(T.ppos[:, 1:32:2], T.I1[:], T.F[:, 0:32:2], False, False, ["F", "I1"], ["ppos"])
-        for h in range(2):
-            for k in range(2):
-                mat(T.ppos[:, h:32:2], T.A3[:], T.F[:, k:32:2], False, False, ["F"] + A3, ["ppos"])
+        even, odd = T.ppos[:, 0:32:2], T.ppos[:, 1:32:2]
+        mat(T.ppos[:, 0:32], T.M1[:], T.F[:], True, False, ["F", "M1"], ["ppos"])
+        mat(even, T.A3[:], T.F[:, 1:32:2], False, False, ["F"] + A3, ["ppos"])
+        mat(odd, T.AI[:], T.F[:, 0:32:2], False, False, ["F", "AI"], ["ppos"])
         for h in range(2):
             mat(T.ppos[:, h:32:2], T.blk[:], T.ir[:, c0 - 1:c0 + 31:2], False, h == 1, ["ir%d" % s, prev, "blk"],
                 ["ppos"])
@@ -370,27 +382,44 @@ def rank_program(g, core, T, topo):
         vts(T.tm[:], T.F[:], 255.0, A.mult, ["F"], ["tm"], (), 1.0, A.add)
         vtt(T.pa[:], T.x1[:], T.tm[:], A.mult, ["x1", "tm"], ["pa"])
         swap(T.pp, "pp", T.pa, ["pa"], 32)
-        if s == 0:
-            vcopy(T.W[:, 16:16 + 16 * VO], T.stw[:, 0:6144].indirect(T.lu[:, 0:VO]), ["lu"], ["WV"], sd)
         vts(T.posu[:], T.ppos[:, 0:32], -8176.0, A.add, ["ppos"], ["posu"], (), 0.0, A.max)
-        wr = ["posu", "wz", "WV"] + ["W%d" % B for B in range(s + 1)]
+        if s == 0:
+            vtr(T.ZK[:], T.pk[:], pk, ["ZK"])
+            vcopy(T.lk[:], T.ZK[:], ["ZK"], ["lk"])
+        else:
+            wr = wr + ["W%d_%d" % (s, k) for k in range(8)]
+        vb = VL if last else VB
         win2 = T.W[:, 0:16 + 2048 * (s + 1)]
-        scopy(T.G2[:, 16 * VB:512], win2.indirect(T.posu[:, VB:32]), wr, ["HS"])
-        vcopy(T.G2[:, 0:16 * VB], win2.indirect(T.posu[:, 0:VB]), wr, ["HV"])
+        scopy(T.G2[:, 16 * vb:512], win2.indirect(T.posu[:, vb:32]), wr, ["HS"])
+        vcopy(T.G2[:, 0:16 * vb], win2.indirect(T.posu[:, 0:vb]), wr, ["HV"])
+        if s == 0:
+            order(1)
         if not last:
-            order(s + 1)
+            vcopy(T.pai[:], T.pa[:], ["pa"], ["pai"])
         vtr(T.T2[:], T.G2[:], ["HV", "HS"], ["T2"])
         if not last:
             vtt(T.x[:], T.T2[:, 0::16], T.pp[:, 0:32], A.add, ["T2", "pp"], ["x"])
+            vts(T.hb[:], T.pai[:], -2048, A.bitwise_and, ["pai"], ["hb"])
         else:
             vtt(T.xl[:], T.T2[:, 0::16], T.pp[:, 0:32], A.add, ["T2", "pp"], ["xl"])
             vtr(T.xlt[:], T.xl[:], ["xl"], ["xlt"])
             spread(T.xlt[:], T.rF[:, me, :], "af%d" % me, ["xlt"])
 
-    lu01 = lists(0, 64, "au", ["of0", "of1"])
-    lu2 = lists(64, 96, "av", ["of2"])
-    scopy(T.SY[:, 0:2 * L], T.lw[:, 0:2048].indirect(T.lst[:, 0:64]), lu01, ["sy01"], lwd)
-    vcopy(T.SY[:, 2 * L:3 * L], T.lw[:, 0:2048].indirect(T.lst[:, 64:96]), lu2, ["sy2"], lwd)
+    def landed(nm, evs, d):
+        if d == me:
+            return [wrote[e][0] for e in evs]
+        count["%s%d" % (nm, d)] = ne
+        return [("%s%d" % (nm, d), ne, "r")]
+
+    names = []
+    for d in [me] + near:
+        dep = landed("av", ["of0", "of1", "of2"], d)
+        for t in range(2):
+            p, o = 64 * t + 16 * me, 32 * d + 16 * t
+            names.append("l%d_%d" % (d, t))
+            D("y", T.lst[o:o + 16, :], T.offs[p:p + 16, :] if d == me else T.rs[p:p + 16, d, :], (), [names[-1]], dep)
+    scopy(T.SY[:, 0:2 * L], T.lw[:, 0:2048].indirect(T.lst[:, 0:64]), names, ["sy01"], lwd)
+    vcopy(T.SY[:, 2 * L:3 * L], T.lw[:, 0:2048].indirect(T.lst[:, 64:96]), names, ["sy2"], lwd)
     D("s", T.syms[:, 0:2 * L], T.SY[2::16, 0:2 * L], ["sy01"])
     D("y", T.syms[:, 2 * L:3 * L], T.SY[2::16, 2 * L:3 * L], ["sy2"])
     i, w = me // 2, me % 2

from concourse.bass import DstId, RemoteDMATransfer
from concourse.mybir import dt, AluOpType, AxisListType, ActivationFunctionType

N, L, S, Q = 4, 512, 3, 1536
SCRATCH = {
    "tx2": ("dram", [4, 128, 32], "int32"),
    "rx2": ("dram", [4, 128, 32], "int32"),
    "tx1": ("dram", [4, 128, 24], "bfloat16"),
    "rx1": ("dram", [4, 128, 24], "bfloat16"),
    "tx0": ("dram", [4, 128, 8], "int32"),
    "rx0": ("dram", [4, 128, 8], "int32"),
    "stin": ("sbuf", [128, 96], "int32"),
    "stb": ("sbuf", [128, 96], "bfloat16"),
    "sx": ("sbuf", [128, 32], "int32"),
    "stw": ("sbuf", [128, 6144], "bfloat16"),
    "win": ("sbuf", [128, 2048], "int32"),
    "mi": ("sbuf", [128, 128], "int32"),
    "mc": ("sbuf", [128, 128], "int32"),
    "mf": ("sbuf", [128, 128], "int32"),
    "sl": ("sbuf", [128, 128], "int32"),
    "slm": ("sbuf", [128, 128], "int32"),
    "qf": ("sbuf", [128, 128], "float32"),
    "qd": ("sbuf", [128, 128], "float32"),
    "qe": ("sbuf", [128, 128], "float32"),
    "li": ("sbuf", [128, 128], "int32"),
    "lf": ("sbuf", [128, 128], "float32"),
    "lw": ("sbuf", [128, 2048], "float32"),
    "pl": ("sbuf", [128, 4, 16], "int32"),
    "pk": ("sbuf", [128, 64], "int32"),
    "Z": ("sbuf", [128, 4, 32], "int32"),
    "ZT": ("sbuf", [128, 128], "int32"),
    "ZK": ("sbuf", [128, 64], "int32"),
    "lu": ("sbuf", [128, 128], "uint16"),
    "lk": ("sbuf", [128, 64], "uint16"),
    "R1": ("sbuf", [128, 512], "bfloat16"),
    "R2": ("sbuf", [128, 512], "bfloat16"),
    "W": ("sbuf", [128, 6160], "bfloat16"),
    "x": ("sbuf", [128, 32], "int32"),
    "offi": ("sbuf", [128, 32], "int32"),
    "offs": ("sbuf", [128, 96], "uint16"),
    "rs": ("sbuf", [128, 4, 96], "uint16"),
    "lst": ("sbuf", [128, 96], "uint16"),
    "SY": ("sbuf", [128, 1536], "float32"),
    "hi": ("sbuf", [128, 32], "int32"),
    "pai": ("sbuf", [128, 32], "int32"),
    "hb": ("sbuf", [128, 32], "int32"),
    "sw": ("sbuf", [128, 64], "float32"),
    "G": ("sbuf", [128, 512], "int32"),
    "TT": ("sbuf", [128, 512], "int32"),
    "Gf": ("sbuf", [128, 512], "float32"),
    "Tf": ("sbuf", [128, 512], "float32"),
    "fm": ("sbuf", [128, 32], "int32"),
    "nn": ("sbuf", [128, 32], "float32"),
    "mm": ("sbuf", [128, 32], "float32"),
    "x1": ("sbuf", [128, 32], "float32"),
    "F": ("sbuf", [128, 32], "bfloat16"),
    "ir": ("sbuf", [128, 128], "bfloat16"),
    "tm": ("sbuf", [128, 32], "float32"),
    "pa": ("sbuf", [128, 32], "float32"),
    "posu": ("sbuf", [128, 32], "uint16"),
    "G2": ("sbuf", [128, 512], "bfloat16"),
    "T2": ("sbuf", [128, 512], "bfloat16"),
    "xl": ("sbuf", [128, 32], "float32"),
    "xlt": ("sbuf", [128, 32], "float32"),
    "rF": ("sbuf", [128, 4, 32], "float32"),
    "onesf": ("sbuf", [128, 128], "float32"),
    "P0": ("sbuf", [128, 128], "float32"),
    "P1": ("sbuf", [128, 128], "float32"),
    "P2": ("sbuf", [128, 128], "float32"),
    "P3": ("sbuf", [128, 128], "float32"),
    "blk": ("sbuf", [128, 128], "bfloat16"),
    "A3": ("sbuf", [128, 128], "bfloat16"),
    "M1": ("sbuf", [128, 128], "bfloat16"),
    "AI": ("sbuf", [128, 128], "bfloat16"),
    "pxs": ("psum", [128, 512], "float32"),
    "pp": ("psum", [128, 512], "float32"),
    "ppos": ("psum", [128, 512], "float32"),
}
NDMA = 104
SEMAPHORES = (["sv", "ss", "sp", "sg", "loc"] + ["d%d" % i for i in range(NDMA)]
              + ["%s%d" % (k, r) for k in ("ab", "aa", "ax", "av", "af") for r in range(N)])

VG = 16
VB = 14
VL = 16
SF = 8
WG = 768


def rank_program(g, core, T, topo):
    me = T.rank_of(core)
    if me is None:
        return
    A = AluOpType
    COPY = ActivationFunctionType.Copy
    queues = {"v": g.vector, "s": g.scalar, "p": g.tensor, "g": g, "y": g.sync}
    own = {"v": "sv", "s": "ss", "p": "sp", "g": "sg"}
    count, known, wrote, read = {}, {}, {}, {}
    ndma = [0]

    def need(q, ev):
        sem, n = ev[0], ev[1]
        if known.get((q, sem), 0) < n:
            queues[q].wait_ge(T.sem[sem], n)
            known[(q, sem)] = n

    def E(q, call, reads=(), writes=(), deps=(), dma=False):
        evs = list(deps)
        for r in reads:
            evs += wrote.get(r, [])
        for w in writes:
            evs += [e for e in wrote.get(w, [])]
            evs += [e for e in read.get(w, []) if e[2] != q or e[0] != own.get(q)]
        for e in evs:
            if q == "p" and e[0] == "sp":
                continue
            need(q, e)
        ins = call()
        if dma:
            sem = "d%d" % ndma[0]
            ndma[0] += 1
            ins.then_inc(T.sem[sem], 16)
            ev = (sem, 16, q)
            count[sem] = 16
        else:
            sem = own[q]
            count[sem] = count.get(sem, 0) + 1
            ins.then_inc(T.sem[sem], 1)
            ev = (sem, count[sem], q)
        for r in reads:
            read.setdefault(r, []).append(ev)
        for w in writes:
            wrote[w] = [ev]
            read[w] = []
        return ev

    def D(q, out, in_, reads=(), writes=(), deps=()):
        return E(q, lambda: queues[q].dma_start(out, in_), reads, writes, deps, True)

    V = g.vector

    def vcopy(out, in_, reads, writes, deps=()):
        return E("v", lambda: V.tensor_copy(out, in_), reads, writes, deps)

    def vfill(ap, c, w):
        return E("v", lambda: V.memset(ap, c), (), [w])

    def vts(out, in0, s1, op0, reads, writes, deps=(), s2=None, op1=None):
        if op1 is None:
            return E("v", lambda: V.tensor_scalar(out, in0, s1, None, op0), reads, writes, deps)
        return E("v", lambda: V.tensor_scalar(out, in0, s1, s2, op0, op1), reads, writes, deps)

    def vtt(out, a, b, op, reads, writes, deps=()):
        return E("v", lambda: V.tensor_tensor(out, a, b, op), reads, writes, deps)

    def vtr(out, in_, reads, writes):
        return E("v", lambda: V.transpose(out, in_), reads, writes)

    def scopy(out, in_, reads, writes, deps=()):
        return E("s", lambda: g.scalar.activation(out, in_, COPY), reads, writes, deps)

    def mat(out, lhsT, rhs, start, stop, reads, writes):
        return E("p", lambda: g.tensor.matmul(out, lhsT, rhs, start, stop), reads, writes)

    cores = list(T.cores)

    def hops(a, b):
        a, b = topo.chip(cores[a]), topo.chip(cores[b])
        return 0 if a == b else (1 if topo.mates(a, b) or topo.same_plane(a, b) else 2)

    def far_of(r):
        return sorted([k for k in range(N) if k != r], key=lambda k: -hops(r, k))

    def common(r):
        f = far_of(r)
        return [e for e in topo.engines(cores[r], cores[f[0]])
                if all(e in topo.engines(cores[r], cores[k]) for k in f)]

    def shares(r, turn):
        e, f = common(r), far_of(r)
        k = len(e) // 4
        e = e[2 * k * turn:] + e[:2 * k * turn]
        return {f[0]: e[0:2 * k], f[1]: e[2 * k:3 * k], f[2]: e[3 * k:4 * k]}

    def bits(es):
        m = 0
        for e in es:
            m |= 1 << e
        return m

    def dst(r):
        ad = topo.addr(cores[r])
        return DstId(rid=ad[0], pnc=ad[1])

    far = far_of(me)
    near = far[::-1]
    ne = len(common(me))
    sent = [0]
    TURN = {"ab": 0, "ax": 1, "aa": 1}

    def scatter(src, out, sem, reads):
        for nm in reads:
            need("g", wrote[nm][0])
        sh = shares(me, TURN[sem])
        g.remote_dma_fused([RemoteDMATransfer(dst_ids=[dst(r)], dma_engine_mask=bits(sh[r]),
                                              remote_sem=T.sem["%s%d" % (sem, me)], srcs=[src[r]], dsts=[out[me]])
                            for r in far], local_sem=T.sem.loc)
        sent[0] += sum([len(sh[r]) for r in far])

    def spread(src, out, sem, reads):
        for nm in reads:
            need("g", wrote[nm][0])
        g.remote_dma_fused([RemoteDMATransfer(dst_ids=[dst(r) for r in far], dma_engine_mask=bits(common(me)),
                                              remote_sem=T.sem[sem], srcs=[src], dsts=[out for r in far])],
                           local_sem=T.sem.loc)
        sent[0] += ne

    D("y", T.tx0[:], T.states[:], (), ["tx0"])
    D("y", T.tx2[:], T.models[:], (), ["tx2"])
    D("s", T.stin[:], T.stock[:], (), ["stin"])
    for a in range(4):
        D("y", T.pl[32 * a:32 * a + 32], T.places[2 * me + a // 2:2 * me + a // 2 + 1, 0:2048], (), ["pl%d" % a])
    own2 = D("y", T.rx2[me], T.models[2 * me:2 * me + 2, :], (), ["own2"])
    own0 = D("y", T.rx0[me], T.states[2 * me:2 * me + 2, :], (), ["own0"])
    D("y", T.li[:], T.letters[:], (), ["li"])

    fw = [E("g", lambda: g.iota(T.win[:, 0:WG], [[1, WG]], 0, 0), (), ["wi"])]
    fs = [vfill(T.stw[:, 0:512], 0.0, "sA")]
    vfill(T.onesf[:], 1.0, "onesf")
    vfill(T.blk[:], 0.0, "blk")
    for t in range(2):
        vfill(T.blk[64 * t:64 * t + 64, 64 * t:64 * t + 64], 1.0, "blk")
    fw.append(vfill(T.win[:, WG:WG + 256], 0, "wa"))
    fl = []
    for k in range(12 - SF, 12):
        fs.append(scopy(T.stw[:, 512 * k:512 * k + 512], T.stw[:, 0:512], ["sA"], ["sB%d" % k]))
    for k in range(4):
        fl.append(scopy(T.lw[:, 512 * k:512 * k + 512], T.lw[:, 0:512] if k else T.stw[:, 0:512], ["lz0" if k else "sA"],
                        ["lz%d" % k]))
    fs.append(fl[0])

    vcopy(T.stb[:], T.stin[:], ["stin"], ["stb"])
    D("y", T.tx1[:], T.stb[:], ["stb"], ["tx1"])
    own1 = D("y", T.rx1[me], T.stb[32 * me:32 * me + 32, :], ["stb"], ["own1"])

    scatter([T.tx0[r] for r in range(N)], T.rx0, "ax", ["tx0"])
    scatter([T.tx2[r] for r in range(N)], T.rx2, "ab", ["tx2"])
    scatter([T.tx1[r] for r in range(N)], T.rx1, "aa", ["tx1"])

    for k, base in enumerate((0, -1000, -16, -1016)):
        out = T["P%d" % k]
        E("g", lambda: g.affine_select(out[:], T.onesf[:], [[-32, 4], [1000, 2], [-1, 16]], A.is_equal, 0.0, base, 1),
          ["onesf"], ["P%d" % k])
        if k == 0:
            E("g", lambda: g.iota(T.sl[:], [[1, 128]], 0, 128), (), ["sl"])
    for a in range(4):
        E("g", lambda: g.affine_select(T.A3[32 * a:32 * a + 32, :], T.blk[32 * a:32 * a + 32, :],
                                       [[0, 2], [1, 2], [2, 32]], A.is_gt, 0.0, -(a % 2), -2), ["blk"], ["A3_%d" % a],
          [("sg", count["sg"], "g")])
    A3 = ["A3_%d" % a for a in range(4)]
    for nm, c in (("M1", 8192.0), ("AI", 1.0)):
        E("g", lambda: g.affine_select(T[nm][:], T.A3[:], [[-1, 128]], A.not_equal, c, 0, 1), A3, [nm])
    E("g", lambda: g.iota(T.W[:, 4112:6160], [[0, 2048]], 0, 0, allow_small_or_imprecise_dtypes=True), (), ["wz2"])

    fw.append(vfill(T.win[:, WG + 256:2048], 0, "wb"))
    fs.append(vfill(T.stw[:, 512:6144 - 512 * SF], 0.0, "sC"))
    vfill(T.ir[:, 0:32], 0.0, "irz")
    vfill(T.W[:, 0:16], 0.0, "wz")
    for w in range(2):
        vcopy(T.Z[:, :, 16 * w:16 * w + 16], T.pl[:], ["pl%d" % a for a in range(4)], ["Z%d" % w])
    for u in range(4):
        vtr(T.ZT[:, u::4], T.Z[:, u, :], ["Z0", "Z1"], ["ZT%d" % u])
    vcopy(T.lu[:], T.ZT[:], ["ZT%d" % u for u in range(4)], ["lu"])
    vcopy(T.lf[:], T.li[:], ["li"], ["lf"])
    vfill(T.W[:, 2064:4112], 0.0, "wz1")
    vts(T.slm[:], T.sl[:], 2047, A.bitwise_and, ["sl"], ["slm"])

    arr = {"ab": [own2], "ax": [own0], "aa": [own1]}
    for r in near:
        for nm in arr:
            n = len(shares(r, TURN[nm])[me])
            count["%s%d" % (nm, r)] = n
            arr[nm].append(("%s%d" % (nm, r), n, "r"))
    wd, sd = [], []
    for t in range(2):
        for w in range(2):
            D("y", T.sx[64 * t:64 * t + 64, 16 * w:16 * w + 16], T.rx0[w::2, 64 * t:64 * t + 64, :],
              (), ["sx%d%d" % (t, w)], arr["ax"])
    for t in range(2):
        wd.append(D("y", T.win[64 * t:64 * t + 64:16, :], T.rx2[:, 64 * t:64 * t + 64, :], (), (), fw + arr["ab"]))
    for u in range(4):
        for t in range(2):
            p = 64 * t + 16 * u
            sd.append(D("y", T.stw[p:p + 1, :], T.rx1[:, 64 * t:64 * t + 64, :], (), (), fs + arr["aa"]))
    for t in range(2):
        D("y", T.mi[64 * t:64 * t + 64, :], T.rx2[:, 64 * t:64 * t + 64, :], (), ["mi%d" % t], arr["ab"])

    pk = []
    for B in range(2):
        for a in range(4):
            for w in range(2):
                o, c = 2048 * (B + 1) + 1024 * (a % 2) + 512 * w, 32 * B + 16 * w
                pk.append("pk%d" % len(pk))
                D("y", T.pk[32 * a:32 * a + 32, c:c + 16], T.places[2 * me + a // 2:2 * me + a // 2 + 1, o:o + 512],
                  (), [pk[-1]])

    lwd = [D("y", T.lw[2::16, :], T.lf[:], ["lf"], (), fl)]

    def second(k, nm):
        lwd.append(D("y", T.lw[k::16, :], T[nm][:], [nm], (), fl))

    def swap(out, w, src, r, n):
        for c in range(2):
            for i in range(2):
                nm = "P%d" % (2 * c + i)
                mat(out[:, c:n:2], T[nm][:], src[:, i:n:2], i == 0, i == 1, r + [nm], [w])

    def order(B):
        src = "R%d" % B
        scopy(T[src][:], T.stw[:, 0:6144].indirect(T.lk[:, 32 * B - 32:32 * B]), ["lk"], [src], sd)
        for t in range(2):
            for u in range(4):
                p = 64 * t + 16 * u
                D("y", T.W[p:p + 1, 16 + 2048 * B:2064 + 2048 * B], T[src][64 * t:64 * t + 64:16, :], [src],
                  ["W%d_%d" % (B, 4 * t + u)], wrote["wz%d" % B])

    vtr(T.x[:], T.sx[:], ["sx00", "sx01", "sx10", "sx11"], ["x"])
    scopy(T.W[:, 16:2064], T.stw[:, 0:6144].indirect(T.lu[:]), ["lu"], ["W0"], sd)
    wr = ["posu", "wz", "W0"]
    for s in range(S):
        last = s == S - 1
        slots = "of%d" % s
        o = 32 * s
        vts(T.offi[:], T.x[:], 2047, A.bitwise_and, ["x"], ["offi"])
        vcopy(T.offs[:, o:o + 32], T.offi[:], ["offi"], [slots])
        if s == 0:
            vts(T.hi[:], T.x[:], 11, A.logical_shift_right, ["x"], ["hi"])
            vts(T.sw[:, 0:32], T.hi[:], 2048.0, A.add, ["hi"], ["sw"])
            vtt(T.sw[:, 32:64], T.hi[:], T.offi[:], A.add, ["hi", "offi"], ["swb"])
            swap(T.pxs, "pxs", T.sw, ["sw", "swb"], 64)
            vcopy(T.G[:], T.win[:, 0:2048].indirect(T.offs[:, o:o + 32]), [slots], ["G"], wd)
            vts(T.mc[:], T.mi[:], 2047, A.bitwise_and, ["mi0", "mi1"], ["mc"])
            vtr(T.TT[:], T.G[:], ["G"], ["TT"])
            vts(T.mf[:], T.mi[:], 11, A.logical_shift_right, ["mi0", "mi1"], ["mf"])
            vts(T.fm[:], T.TT[:, 0::16], 11, A.logical_shift_right, ["TT"], ["fm"])
            vtt(T.nn[:], T.pxs[:, 32:64], T.TT[:, 0::16], A.subtract, ["pxs", "TT"], ["nn"])
            vtt(T.mm[:], T.fm[:], T.pxs[:, 0:32], A.mult, ["fm", "pxs"], ["mm"])
            vtt(T.qd[:], T.slm[:], T.mc[:], A.subtract, ["slm", "mc"], ["qd"])
            second(1, "qd")
            vtt(T.x1[:], T.mm[:], T.nn[:], A.add, ["mm", "nn"], ["x1"])
            vts(T.qf[:], T.mf[:], 1.0, A.add, ["mf"], ["qf"], (), 1.0 / 2048, A.mult)
            second(0, "qf")
            vts(T.F[:], T.x1[:], 4096.0, A.is_lt, ["x1"], ["F"])
        else:
            lw = T.lw[:, 0:2048]
            scopy(T.Gf[:, 16 * VG:512], lw.indirect(T.offs[:, o + VG:o + 32]), [slots], ["GS"], lwd)
            if not last:
                order(2)
            vcopy(T.Gf[:, 0:16 * VG], lw.indirect(T.offs[:, o:o + VG]), [slots], ["GV"], lwd)
            if last:
                spread(T.offs[:], T.rs[:, me, :], "av%d" % me, ["of0", "of1", "of2"])
            vtr(T.Tf[:], T.Gf[:], ["GV", "GS"], ["Tf"])
            vtt(T.mm[:], T.Tf[:, 0::16], T.hb[:], A.mult, ["Tf", "hb"], ["mm"])
            vtt(T.F[:], T.mm[:], T.Tf[:, 3::16], A.is_lt, ["mm", "Tf"], ["F"])
            vtt(T.x1[:], T.mm[:], T.Tf[:, 1::16], A.add, ["mm", "Tf"], ["x1"])
        c0 = 32 + 32 * s
        prev = "irz" if s == 0 else "ir%d" % (s - 1)
        E("v", lambda: V.tensor_tensor_scan(T.ir[:, c0:c0 + 32], T.F[:], T.ir[:, 0:32], T.ir[:, c0 - 1:c0], A.add, A.add),
          ["F", "irz", prev], ["ir%d" % s])
        if s == 0:
            vts(T.qe[:], T.qd[:], -1.0, A.mult, ["qd"], ["qe"], (), 4096.0, A.add)
            second(3, "qe")

        even, odd = T.ppos[:, 0:32:2], T.ppos[:, 1:32:2]
        mat(T.ppos[:, 0:32], T.M1[:], T.F[:], True, False, ["F", "M1"], ["ppos"])
        mat(even, T.A3[:], T.F[:, 1:32:2], False, False, ["F"] + A3, ["ppos"])
        mat(odd, T.AI[:], T.F[:, 0:32:2], False, False, ["F", "AI"], ["ppos"])
        for h in range(2):
            mat(T.ppos[:, h:32:2], T.blk[:], T.ir[:, c0 - 1:c0 + 31:2], False, h == 1, ["ir%d" % s, prev, "blk"],
                ["ppos"])

        vts(T.tm[:], T.F[:], 255.0, A.mult, ["F"], ["tm"], (), 1.0, A.add)
        vtt(T.pa[:], T.x1[:], T.tm[:], A.mult, ["x1", "tm"], ["pa"])
        swap(T.pp, "pp", T.pa, ["pa"], 32)
        vts(T.posu[:], T.ppos[:, 0:32], -8176.0, A.add, ["ppos"], ["posu"], (), 0.0, A.max)
        if s == 0:
            vtr(T.ZK[:], T.pk[:], pk, ["ZK"])
            vcopy(T.lk[:], T.ZK[:], ["ZK"], ["lk"])
        else:
            wr = wr + ["W%d_%d" % (s, k) for k in range(8)]
        vb = VL if last else VB
        win2 = T.W[:, 0:16 + 2048 * (s + 1)]
        scopy(T.G2[:, 16 * vb:512], win2.indirect(T.posu[:, vb:32]), wr, ["HS"])
        vcopy(T.G2[:, 0:16 * vb], win2.indirect(T.posu[:, 0:vb]), wr, ["HV"])
        if s == 0:
            order(1)
        if not last:
            vcopy(T.pai[:], T.pa[:], ["pa"], ["pai"])
        vtr(T.T2[:], T.G2[:], ["HV", "HS"], ["T2"])
        if not last:
            vtt(T.x[:], T.T2[:, 0::16], T.pp[:, 0:32], A.add, ["T2", "pp"], ["x"])
            vts(T.hb[:], T.pai[:], -2048, A.bitwise_and, ["pai"], ["hb"])
        else:
            vtt(T.xl[:], T.T2[:, 0::16], T.pp[:, 0:32], A.add, ["T2", "pp"], ["xl"])
            vtr(T.xlt[:], T.xl[:], ["xl"], ["xlt"])
            spread(T.xlt[:], T.rF[:, me, :], "af%d" % me, ["xlt"])

    def landed(nm, evs, d):
        if d == me:
            return [wrote[e][0] for e in evs]
        count["%s%d" % (nm, d)] = ne
        return [("%s%d" % (nm, d), ne, "r")]

    names = []
    for d in [me] + near:
        dep = landed("av", ["of0", "of1", "of2"], d)
        for t in range(2):
            p, o = 64 * t + 16 * me, 32 * d + 16 * t
            names.append("l%d_%d" % (d, t))
            D("y", T.lst[o:o + 16, :], T.offs[p:p + 16, :] if d == me else T.rs[p:p + 16, d, :], (), [names[-1]], dep)
    scopy(T.SY[:, 0:2 * L], T.lw[:, 0:2048].indirect(T.lst[:, 0:64]), names, ["sy01"], lwd)
    vcopy(T.SY[:, 2 * L:3 * L], T.lw[:, 0:2048].indirect(T.lst[:, 64:96]), names, ["sy2"], lwd)
    D("s", T.syms[:, 0:2 * L], T.SY[2::16, 0:2 * L], ["sy01"])
    D("y", T.syms[:, 2 * L:3 * L], T.SY[2::16, 2 * L:3 * L], ["sy2"])
    i, w = me // 2, me % 2
    for d in [me] + near:
        dep = landed("af", ["xlt"], d)
        for t, q in ((0, "y"), (1, "s")):
            p = 64 * t + 32 * i
            xs = T.xlt[p:p + 32, 16 * w:16 * w + 16] if d == me else T.rF[p:p + 32, d, 16 * w:16 * w + 16]
            D(q, T.last[2 * d + t:2 * d + t + 1, :], xs, (), (), dep)

    for sem in sorted(count):
        if max([known.get((q, sem), 0) for q in queues]) < count[sem]:
            need("y", (sem, count[sem], ""))
    g.wait_ge(T.sem.loc, sent[0])
